import numpy as np
import ml_dtypes


def mxq(x, axis, fmt="e4m3"):
    dtype, down = {"e4m3": (ml_dtypes.float8_e4m3fn, 7), "e5m2": (ml_dtypes.float8_e5m2, 14)}[fmt]
    v = np.moveaxis(np.asarray(x, np.float32).astype(ml_dtypes.bfloat16).astype(np.float64), axis, -1)
    blocks = v.reshape(v.shape[:-1] + (-1, 32))
    amax = np.abs(blocks).max(-1, keepdims=True)
    byte = np.maximum(np.where(amax > 0, np.frexp(amax)[1] - 1 + 127, 0) - down, 1)
    scale = np.exp2(byte - 127.0)
    codes = (blocks / scale).astype(np.float32).astype(dtype).astype(np.float64)
    return np.moveaxis((codes * scale).reshape(v.shape), -1, axis)


WIDE = False


def mx_kscale(k):
    if not WIDE:
        return np.ones(k)
    levels = np.array([10, -10, 5, -5, 0])
    if k % 512:
        return np.exp2(np.random.permutation(np.resize(levels, k // 32))).repeat(32)
    a = np.empty((k // 512, 16))
    for p in range(k // 512):
        a[p, :8] = np.random.permutation(np.resize(levels, 8))
        for g in range(8):
            far = levels[np.abs(levels - a[p, g]) >= 10]
            a[p, g + 8] = far[np.random.randint(len(far))]
    return np.exp2(a.ravel()).repeat(32)


def f64(x):
    return np.asarray(x).astype(np.float64)


def striped(idx):
    return np.tile(idx.reshape(-1, 16).T, (8, 1)).astype(np.uint16)


def unstriped(offs):
    return offs[:16].T.reshape(-1).astype(np.int64)


E2M1 = np.array([0.0, 0.5, 1.0, 1.5, 2.0, 3.0, 4.0, 6.0, -0.0, -0.5, -1.0, -1.5, -2.0, -3.0, -4.0, -6.0])


def pack_weight(w, fmt):
    k, n = w.shape
    w = f64(np.asarray(w, np.float32).astype(ml_dtypes.bfloat16)).reshape(k // 32, 32, n)
    amax = np.abs(w).max(1)
    if fmt == "e4m3":
        byte = np.frexp(amax)[1] - 1 + 127 - 7
    else:
        mant, ex = np.frexp(amax / 6.0)
        byte = np.where(mant > 0.5, ex, ex - 1) + 127
    byte = np.clip(np.where(amax > 0, byte, 1), 1, 254)
    scaled = (w * np.exp2(127.0 - byte)[:, None, :]).reshape(k, n).astype(np.float32)
    by_word = np.ascontiguousarray(scaled.reshape(k // 512, 128, 4, n).transpose(0, 1, 3, 2))
    if fmt == "e4m3":
        words = by_word.astype(ml_dtypes.float8_e4m3fn).view(np.uint8)
    else:
        c = by_word.astype(ml_dtypes.float4_e2m1fn).view(np.uint8) & 0xF
        words = (c[..., 0::2] | (c[..., 1::2] << 4)).reshape(k // 512, 128, 2 * n)
    return np.ascontiguousarray(words), np.ascontiguousarray(byte.astype(np.uint8).reshape(k // 512, 16, n))


def unpack_weight(words, scales, fmt):
    g, _, n = scales.shape
    words = np.ascontiguousarray(words).reshape(g, 128, n, -1)
    if fmt == "e4m3":
        vals = words.view(ml_dtypes.float8_e4m3fn).astype(np.float64)
    else:
        nib = np.empty((g, 128, n, 4), np.uint8)
        nib[..., 0::2] = words & 0xF
        nib[..., 1::2] = words >> 4
        vals = E2M1[nib]
    vals = vals * np.repeat(np.exp2(scales.astype(np.float64) - 127.0), 8, axis=1)[..., None]
    return vals.transpose(0, 1, 3, 2).reshape(g * 512, n)


def silu(v):
    return v / (1.0 + np.exp(-np.maximum(v, -700.0)))


K, T, E, C, N = 1536, 1024, 12, 256, 128
TOP = 3
K8 = 512


def by_expert(wq, xq):
    return np.concatenate([wq[e].T @ xq[:, e * C:(e + 1) * C] for e in range(E)], axis=1)


def setup_inputs():
    n = np.random.standard_normal
    s = mx_kscale(K)[:, None]
    deal = np.repeat(np.arange(E), C).reshape(TOP, T)[:, np.random.permutation(T)]
    deal = np.take_along_axis(deal, np.argsort(np.random.rand(TOP, T), axis=0), axis=0)
    for _ in range(8):
        s_, t_ = np.random.permutation(T).reshape(2, -1); r = np.random.randint(TOP, size=T // 2); x, y = deal[r, s_].copy(), deal[r, t_].copy()
        ok = ~((deal[:, s_] == y).any(0) | (deal[:, t_] == x).any(0)); deal[r[ok], s_[ok]] = y[ok]; deal[r[ok], t_[ok]] = x[ok]
    order = np.lexsort((np.random.rand(TOP * T), deal.reshape(-1)))
    slot_token = order % T; pos = np.empty(TOP * T, np.int64); pos[order] = np.arange(TOP * T); pos = pos.reshape(TOP, T)
    g = np.random.uniform(0.5, 1.5, (TOP, T)); g = g / g.sum(0)
    w = n((E, K, N)) / np.sqrt(K) / s[None]
    w8 = [pack_weight(m[:K8], "e4m3") for m in w]
    w4 = [pack_weight(m[K8:], "e2m1") for m in w]
    return {
        "xT": (n((K, T)) * s).astype(np.float32),
        "w8_words": np.stack([m[0] for m in w8]),
        "w8_scales": np.stack([m[1] for m in w8]),
        "w4_words": np.stack([m[0] for m in w4]),
        "w4_scales": np.stack([m[1] for m in w4]),
        "b": (0.3 * n((N, E))).astype(np.float32),
        "gate": np.stack([np.tile(r, (N, 1)) for r in g]).astype(np.float32),
        "offs": striped(slot_token),
        "pos1": striped(pos[0]),
        "pos2": striped(pos[1]),
        "pos3": striped(pos[2]),
    }


def reference(xT, w8_words, w8_scales, w4_words, w4_scales, b, gate, offs, pos1, pos2, pos3):
    idx = unstriped(offs)
    w = np.stack([np.concatenate([unpack_weight(w8_words[e], w8_scales[e], "e4m3"), unpack_weight(w4_words[e], w4_scales[e], "e2m1")]) for e in range(E)])
    xq = mxq(f64(xT)[:, idx], 0, "e4m3")
    y = by_expert(w, xq)
    y = silu(y + np.repeat(f64(b), C, axis=1))
    return sum(f64(gate[r]) * y[:, unstriped(p)] for r, p in enumerate((pos1, pos2, pos3)))

@@ -1,0 +1,197 @@
+from contextlib import ExitStack
+
+import concourse.mybir as mybir
+
+K, T, E, C, N = 1536, 1024, 12, 256, 128
+TOP = 3
+S = E * C
+PASSES = 3
+P = 128
+FLOPS = 2 * S * K * N
+
+F32 = mybir.dt.float32
+BF16 = mybir.dt.bfloat16
+I32 = mybir.dt.int32
+U32 = mybir.dt.uint32
+U16 = mybir.dt.uint16
+U8 = mybir.dt.uint8
+FP8X4 = mybir.dt.float8_e4m3fn_x4
+FP4X4 = mybir.dt.float4_e2m1fn_x4
+COPY = mybir.ActivationFunctionType.Copy
+SILU = mybir.ActivationFunctionType.Silu
+MULT = mybir.AluOpType.mult
+
+CUT = 1536
+PLANE = (4, 0, 8)
+
+
+def tile_moe_tk_lin_silu_kernel(
+    tc, xT, w8_words, w8_scales, w4_words, w4_scales, b, gate, offs, pos1, pos2, pos3, out
+):
+    nc = tc.nc
+    with ExitStack() as ctx:
+        held = ctx.enter_context(tc.tile_pool(name="held", bufs=1))
+        psum = ctx.enter_context(tc.psum_pool(name="psum", bufs=8))
+
+        offs_t = held.tile([P, S // 16], U16, name="offs_t")
+        pos_t = [held.tile([P, T // 16], U16, name=f"pos_t{r}") for r in range(TOP)]
+
+        planes = held.tile([P, 2 * T], U8, name="planes", align_bytes=64)
+        codes = [
+            held.tile([P, 2 * T if a < PASSES - 1 else T], U32, name=f"codes{a}", align_bytes=64) for a in range(PASSES)
+        ]
+        low = held.tile([P, S], U8, name="low", align_bytes=64)
+        ws8 = held.tile([P, E, N], U8, name="ws8", align_bytes=64)
+        ws4 = held.tile([P, 2 * E, N], U8, name="ws4", align_bytes=64)
+        warm = held.tile([P, 1], F32, name="warm")
+        nc.vector.memset(warm[:], 0.0)
+        nc.gpsimd.memset(planes[:].bitcast(I32), 0)
+        nc.gpsimd.memset(ws8[:].rearrange("p e n -> p (e n)").bitcast(I32), 0)
+        nc.gpsimd.memset(ws4[:].rearrange("p e n -> p (e n)").bitcast(I32), 0)
+        nc.gpsimd.memset(low[:].bitcast(I32), 0)
+        warm_out = held.tile([P, 1], F32, name="warm_out")
+        nc.scalar.activation(out=warm_out[:], in_=warm[:], func=SILU)
+
+        chunks = [(0, t0, 256) for t0 in range(0, T, 256)] + [(a, t0, 512) for a in (1, 2) for t0 in (0, 512)]
+        raw = {}
+        for a, t0, n in chunks:
+            r = held.tile([P, 4, n], F32, name=f"raw{a}_{t0}")
+            nc.sync.dma_start(
+                out=r[:], in_=xT[512 * a : 512 * a + 512, t0 : t0 + n].rearrange("(p j) t -> p j t", j=4)
+            )
+            raw[a, t0] = r
+            if a == 0 and t0 == 768:
+                nc.sync.dma_start(offs_t[:], offs)
+        for q in range(4):
+            nc.sync.dma_start(
+                out=ws8[32 * q : 32 * q + 4, :, :].bitcast(I32),
+                in_=w8_scales[:, 0, 4 * q : 4 * q + 4, :].rearrange("e q n -> q e n").bitcast(I32),
+            )
+            nc.sync.dma_start(
+                out=ws4[32 * q : 32 * q + 4, :, :].bitcast(I32),
+                in_=w4_scales[:, :, 4 * q : 4 * q + 4, :].rearrange("e a q n -> q (e a) n").bitcast(I32),
+            )
+        w8 = held.tile([P, E, 4 * N], U8, name="w8", align_bytes=64)
+        nc.sync.dma_start(out=w8[:].bitcast(I32), in_=w8_words.rearrange("e a p n r -> p (e a) (n r)").bitcast(I32))
+        w4 = held.tile([P, 2 * E, 2 * N], U8, name="w4", align_bytes=64)
+        nc.sync.dma_start(out=w4[:].bitcast(I32), in_=w4_words.rearrange("e a p m -> p (e a) m").bitcast(I32))
+        bias = held.tile([P, E], F32, name="bias")
+        nc.sync.dma_start(out=bias[:], in_=b)
+        for r, pos in enumerate((pos1, pos2, pos3)):
+            nc.sync.dma_start(pos_t[r][:], pos)
+
+        HELD_BACK = 2304
+        slot_codes = [
+            held.tile([P, HELD_BACK if a == 1 else S], U32, name=f"slot_codes{a}", align_bytes=64) for a in range(PASSES)
+        ]
+        slot_planes = held.tile([P, S], U8, name="slot_planes", align_bytes=64)
+
+        def gather_codes(a, s0, s1):
+            nc.vector.tensor_copy(out=slot_codes[a][:, s0:s1], in_=codes[a][:].indirect(offs_t[:, s0 // 16 : s1 // 16]))
+
+        def round_and_quantise(a, t0, n, on_scalar):
+            grouped = held.tile([P, n, 4], BF16, name=f"grouped{a}_{t0}", tag={(2, 0): "late", (2, 512): "later"}.get((a, t0), f"grouped{a}_{t0}"), align_bytes=64)
+            v = n - on_scalar
+            if on_scalar:
+                nc.scalar.activation(
+                    out=grouped[:, v:n, :].rearrange("p (c i) j -> p c j i", i=4),
+                    in_=raw[a, t0][:, :, v:n].rearrange("p j (c i) -> p c j i", i=4),
+                    func=COPY,
+                )
+            if v:
+                nc.vector.tensor_copy(
+                    out=grouped[:, 0:v, :].rearrange("p (c i) j -> p c j i", i=4),
+                    in_=raw[a, t0][:, :, 0:v].rearrange("p j (c i) -> p c j i", i=4),
+                )
+            for u0, u1 in ((0, v), (v, n)):
+                if u0 < u1:
+                    nc.vector.quantize_mx(
+                        out=codes[a][:, t0 + u0 : t0 + u1].bitcast(FP8X4),
+                        scales=planes[PLANE[a] : P, t0 + u0 : t0 + u1],
+                        in_=grouped[:, u0:u1, :].rearrange("p t j -> p (t j)"),
+                    )
+
+        round_and_quantise(0, 0, 256, 0)
+        round_and_quantise(0, 256, 256, 256)
+        round_and_quantise(0, 512, 256, 0)
+        round_and_quantise(0, 768, 256, 128)
+        gather_codes(0, 0, 1536)
+        gather_codes(0, 1536, 2688)
+        round_and_quantise(1, 0, 512, 512)
+        round_and_quantise(1, 512, 512, 512)
+        gather_codes(0, 2688, 3072)
+        gather_codes(1, 0, 1536)
+        gather_codes(1, 1536, 2304)
+        round_and_quantise(2, 0, 512, 512)
+        round_and_quantise(2, 512, 512, 512)
+        gates = held.tile([P, TOP, T], F32, name="gates", tag="late", align_bytes=64)
+        nc.scalar.dma_start(out=gates[:], in_=gate.rearrange("r p t -> p r t"))
+
+        def gather_bytes(s0, s1):
+            nc.vector.tensor_copy(out=slot_planes[:, s0:s1], in_=planes[:].indirect(offs_t[:, s0 // 16 : s1 // 16]))
+            for q in range(4):
+                nc.sync.dma_start(
+                    out=low[32 * q : 32 * q + 4, s0:s1].bitcast(I32),
+                    in_=slot_planes[32 * q + 8 : 32 * q + 12, s0:s1].bitcast(I32),
+                )
+
+        gather_bytes(0, 768)
+        gather_codes(2, 0, 768)
+        gather_bytes(768, 2304)
+        gather_codes(2, 768, 1536)
+        gather_bytes(2304, 3072)
+        gather_codes(2, 1536, 2304)
+        late_codes = held.tile([P, S - HELD_BACK], U32, name="late_codes", tag="later", align_bytes=64)
+        nc.vector.tensor_copy(out=late_codes[:], in_=codes[1][:].indirect(offs_t[:, HELD_BACK // 16 : S // 16]))
+        gather_codes(2, 2304, 2816)
+        gather_codes(2, 2816, 2944)
+        gather_codes(2, 2944, 3072)
+
+        y = held.tile([P, S], F32, name="y")
+        for s0 in range(0, S, 128):
+            e = s0 // C
+            cols = slice(s0, s0 + 128)
+            acc = psum.tile([P, 128], F32, name="acc")
+            for a in range(PASSES):
+                if a == 0:
+                    lhsT, lhsT_scale = w8[:, e, :].bitcast(FP8X4), ws8[:, e, :]
+                else:
+                    m = 2 * e + a - 1
+                    lhsT, lhsT_scale = w4[:, m, :].bitcast(FP4X4), ws4[:, m, :]
+                nc.tensor.matmul_mx(
+                    out=acc[:],
+                    lhsT=lhsT,
+                    lhsT_scale=lhsT_scale,
+                    rhs=(
+                        late_codes[:, s0 - HELD_BACK : s0 - HELD_BACK + 128]
+                        if a == 1 and s0 >= HELD_BACK
+                        else slot_codes[a][:, cols]
+                    ).bitcast(FP8X4),
+                    rhs_scale=low[:, cols] if a == 2 else slot_planes[PLANE[a] : P, cols],
+                    start=(a == 0),
+                    stop=(a == PASSES - 1),
+                )
+            nc.scalar.activation(out=y[:, cols], in_=acc[:], func=SILU, bias=bias[:, e : e + 1])
+
+        parts = [held.tile([P, T], F32, name=f"part{r}") for r in range(TOP)]
+        total = held.tile([P, T], F32, name="total")
+        result = held.tile([P, T], F32, name="result")
+
+        def fetch(r, t0, t1):
+            nc.vector.tensor_tensor(
+                parts[r][:, t0:t1], y[:].indirect(pos_t[r][:, t0 // 16 : t1 // 16]), gates[:, r, t0:t1], MULT
+            )
+
+        def finish(t0, t1):
+            nc.vector.tensor_add(result[:, t0:t1], total[:, t0:t1], parts[2][:, t0:t1])
+            nc.sync.dma_start(out=out[:, t0:t1], in_=result[:, t0:t1])
+
+        fetch(0, 0, T)
+        fetch(1, 0, T)
+        fetch(2, 0, 512)
+        nc.vector.tensor_add(total[:], parts[0][:], parts[1][:])
+        fetch(2, 512, 768)
+        finish(0, 512)
+        fetch(2, 768, T)
+        finish(512, 768)
+        finish(768, T)

@@ -1,6 +1,7 @@
 from contextlib import ExitStack
 
 import concourse.mybir as mybir
+from concourse.masks import make_identity
 
 K, T, E, C, N = 1536, 1024, 12, 256, 128
 TOP = 3
@@ -51,6 +52,9 @@ def tile_moe_tk_lin_silu_kernel(
         nc.gpsimd.memset(low[:].bitcast(I32), 0)
         warm_out = held.tile([P, 1], F32, name="warm_out")
         nc.scalar.activation(out=warm_out[:], in_=warm[:], func=SILU)
+
+        identity = held.tile([P, P], F32, name="identity")
+        make_identity(nc, identity[:])
 
         chunks = [(0, t0, 256) for t0 in range(0, T, 256)] + [(a, t0, 512) for a in (1, 2) for t0 in (0, 512)]
         raw = {}
@@ -174,24 +178,45 @@ def tile_moe_tk_lin_silu_kernel(
             nc.scalar.activation(out=y[:, cols], in_=acc[:], func=SILU, bias=bias[:, e : e + 1])
 
         parts = [held.tile([P, T], F32, name=f"part{r}") for r in range(TOP)]
-        total = held.tile([P, T], F32, name="total")
-        result = held.tile([P, T], F32, name="result")
+        ON_VECTOR = 768
+        total = held.tile([P, T - ON_VECTOR], F32, name="total")
+        last = held.tile([P, T - ON_VECTOR], F32, name="last")
 
         def fetch(r, t0, t1):
             nc.vector.tensor_tensor(
                 parts[r][:, t0:t1], y[:].indirect(pos_t[r][:, t0 // 16 : t1 // 16]), gates[:, r, t0:t1], MULT
             )
 
-        def finish(t0, t1):
-            nc.vector.tensor_add(result[:, t0:t1], total[:, t0:t1], parts[2][:, t0:t1])
-            nc.sync.dma_start(out=out[:, t0:t1], in_=result[:, t0:t1])
+        def combine_on_tensor(t0, t1, queue):
+            n = t1 - t0
+            turned = psum.tile([P, n], F32, name="acc")
+            for r in range(TOP):
+                fetch(r, t0, t1)
+                for u in range(0, n, P):
+                    nc.tensor.matmul(
+                        turned[:, u : u + P],
+                        lhsT=parts[r][:, t0 + u : t0 + u + P],
+                        rhs=identity[:],
+                        is_transpose=True,
+                        start=(r == 0 and u == 0),
+                        stop=(r == TOP - 1 and u == n - P),
+                    )
+            sums = held.tile([P, n], F32, name=f"sums{t0}")
+            nc.scalar.copy(out=sums[:], in_=turned[:])
+            back = psum.tile([P, n], F32, name="acc")
+            for u in range(0, n, P):
+                nc.tensor.transpose(back[:, u : u + P], sums[:, u : u + P], identity[:])
+            result = held.tile([P, n], F32, name=f"result{t0}")
+            nc.scalar.copy(out=result[:], in_=back[:])
+            queue.dma_start(out=out[:, t0:t1], in_=result[:])
 
-        fetch(0, 0, T)
-        fetch(1, 0, T)
-        fetch(2, 0, 512)
-        nc.vector.tensor_add(total[:], parts[0][:], parts[1][:])
-        fetch(2, 512, 768)
-        finish(0, 512)
-        fetch(2, 768, T)
-        finish(512, 768)
-        finish(768, T)
+        combine_on_tensor(0, 512, nc.sync)
+        combine_on_tensor(512, ON_VECTOR, nc.scalar)
+        fetch(0, ON_VECTOR, T)
+        fetch(1, ON_VECTOR, T)
+        fetch(2, ON_VECTOR, 896)
+        nc.vector.tensor_add(total[:], parts[0][:, ON_VECTOR:T], parts[1][:, ON_VECTOR:T])
+        fetch(2, 896, T)
+        nc.vector.tensor_add(last[:, 0:128], total[:, 0:128], parts[2][:, ON_VECTOR:896])
+        nc.vector.tensor_add(last[:, 128:256], total[:, 128:256], parts[2][:, 896:T])
+        nc.sync.dma_start(out=out[:, ON_VECTOR:T], in_=last[:])

@@ -46,10 +46,10 @@ def tile_moe_tk_lin_silu_kernel(
         ws4 = held.tile([P, 2 * E, N], U8, name="ws4", align_bytes=64)
         warm = held.tile([P, 1], F32, name="warm")
         nc.vector.memset(warm[:], 0.0)
-        nc.gpsimd.memset(planes[:].bitcast(I32), 0)
-        nc.gpsimd.memset(ws8[:].rearrange("p e n -> p (e n)").bitcast(I32), 0)
-        nc.gpsimd.memset(ws4[:].rearrange("p e n -> p (e n)").bitcast(I32), 0)
-        nc.gpsimd.memset(low[:].bitcast(I32), 0)
+        nc.vector.memset(planes[:].bitcast(I32), 0)
+        nc.vector.memset(ws8[:].rearrange("p e n -> p (e n)").bitcast(I32), 0)
+        nc.vector.memset(ws4[:].rearrange("p e n -> p (e n)").bitcast(I32), 0)
+        nc.vector.memset(low[:].bitcast(I32), 0)
         warm_out = held.tile([P, 1], F32, name="warm_out")
         nc.scalar.activation(out=warm_out[:], in_=warm[:], func=SILU)
 
@@ -178,7 +178,7 @@ def tile_moe_tk_lin_silu_kernel(
             nc.scalar.activation(out=y[:, cols], in_=acc[:], func=SILU, bias=bias[:, e : e + 1])
 
         parts = [held.tile([P, T], F32, name=f"part{r}") for r in range(TOP)]
-        ON_VECTOR = 768
+        ON_VECTOR = 512
         total = held.tile([P, T - ON_VECTOR], F32, name="total")
         last = held.tile([P, T - ON_VECTOR], F32, name="last")
 
@@ -187,7 +187,7 @@ def tile_moe_tk_lin_silu_kernel(
                 parts[r][:, t0:t1], y[:].indirect(pos_t[r][:, t0 // 16 : t1 // 16]), gates[:, r, t0:t1], MULT
             )
 
-        def combine_on_tensor(t0, t1, queue):
+        def combine_on_tensor(t0, t1):
             n = t1 - t0
             turned = psum.tile([P, n], F32, name="acc")
             for r in range(TOP):
@@ -208,15 +208,18 @@ def tile_moe_tk_lin_silu_kernel(
                 nc.tensor.transpose(back[:, u : u + P], sums[:, u : u + P], identity[:])
             result = held.tile([P, n], F32, name=f"result{t0}")
             nc.scalar.copy(out=result[:], in_=back[:])
-            queue.dma_start(out=out[:, t0:t1], in_=result[:])
+            nc.sync.dma_start(out=out[:, t0:t1], in_=result[:])
 
-        combine_on_tensor(0, 512, nc.sync)
-        combine_on_tensor(512, ON_VECTOR, nc.scalar)
+        def finish(t0, t1):
+            u = slice(t0 - ON_VECTOR, t1 - ON_VECTOR)
+            nc.vector.tensor_add(last[:, u], total[:, u], parts[2][:, t0:t1])
+            nc.sync.dma_start(out=out[:, t0:t1], in_=last[:, u])
+
+        combine_on_tensor(0, ON_VECTOR)
         fetch(0, ON_VECTOR, T)
         fetch(1, ON_VECTOR, T)
-        fetch(2, ON_VECTOR, 896)
+        fetch(2, ON_VECTOR, 768)
         nc.vector.tensor_add(total[:], parts[0][:, ON_VECTOR:T], parts[1][:, ON_VECTOR:T])
-        fetch(2, 896, T)
-        nc.vector.tensor_add(last[:, 0:128], total[:, 0:128], parts[2][:, ON_VECTOR:896])
-        nc.vector.tensor_add(last[:, 128:256], total[:, 128:256], parts[2][:, 896:T])
-        nc.sync.dma_start(out=out[:, ON_VECTOR:T], in_=last[:])
+        fetch(2, 768, T)
+        finish(ON_VECTOR, 768)
+        finish(768, T)

@@ -208,7 +208,7 @@ def tile_moe_tk_lin_silu_kernel(
                 nc.tensor.transpose(back[:, u : u + P], sums[:, u : u + P], identity[:])
             result = held.tile([P, n], F32, name=f"result{t0}")
             nc.scalar.copy(out=result[:], in_=back[:])
-            nc.sync.dma_start(out=out[:, t0:t1], in_=result[:])
+            nc.scalar.dma_start(out=out[:, t0:t1], in_=result[:])
 
         def finish(t0, t1):
             u = slice(t0 - ON_VECTOR, t1 - ON_VECTOR)

@@ -56,7 +56,7 @@ def tile_moe_tk_lin_silu_kernel(
         identity = held.tile([P, P], F32, name="identity")
         make_identity(nc, identity[:])
 
-        chunks = [(0, t0, 256) for t0 in range(0, T, 256)] + [(a, t0, 512) for a in (1, 2) for t0 in (0, 512)]
+        chunks = [(0, 0, 512), (0, 512, 256), (0, 768, 256)] + [(a, t0, 512) for a in (1, 2) for t0 in (0, 512)]
         raw = {}
         for a, t0, n in chunks:
             r = held.tile([P, 4, n], F32, name=f"raw{a}_{t0}")
@@ -115,9 +115,8 @@ def tile_moe_tk_lin_silu_kernel(
                         in_=grouped[:, u0:u1, :].rearrange("p t j -> p (t j)"),
                     )
 
-        round_and_quantise(0, 0, 256, 0)
-        round_and_quantise(0, 256, 256, 256)
-        round_and_quantise(0, 512, 256, 0)
+        round_and_quantise(0, 0, 512, 256)
+        round_and_quantise(0, 512, 256, 128)
         round_and_quantise(0, 768, 256, 128)
         gather_codes(0, 0, 1536)
         gather_codes(0, 1536, 2688)
@@ -188,27 +187,30 @@ def tile_moe_tk_lin_silu_kernel(
             )
 
         def combine_on_tensor(t0, t1):
-            n = t1 - t0
-            turned = psum.tile([P, n], F32, name="acc")
+            halves = range(t0, t1, 256)
+            turned = {h: psum.tile([P, 256], F32, name="acc") for h in halves}
             for r in range(TOP):
                 fetch(r, t0, t1)
-                for u in range(0, n, P):
-                    nc.tensor.matmul(
-                        turned[:, u : u + P],
-                        lhsT=parts[r][:, t0 + u : t0 + u + P],
-                        rhs=identity[:],
-                        is_transpose=True,
-                        start=(r == 0 and u == 0),
-                        stop=(r == TOP - 1 and u == n - P),
-                    )
-            sums = held.tile([P, n], F32, name=f"sums{t0}")
-            nc.scalar.copy(out=sums[:], in_=turned[:])
-            back = psum.tile([P, n], F32, name="acc")
-            for u in range(0, n, P):
-                nc.tensor.transpose(back[:, u : u + P], sums[:, u : u + P], identity[:])
-            result = held.tile([P, n], F32, name=f"result{t0}")
-            nc.scalar.copy(out=result[:], in_=back[:])
-            nc.scalar.dma_start(out=out[:, t0:t1], in_=result[:])
+                for h in halves:
+                    for u in (0, P):
+                        nc.tensor.matmul(
+                            turned[h][:, u : u + P],
+                            lhsT=parts[r][:, h + u : h + u + P],
+                            rhs=identity[:],
+                            is_transpose=True,
+                            start=(r == 0 and u == 0),
+                            stop=(r == TOP - 1 and u == P),
+                        )
+            sums = {h: held.tile([P, 256], F32, name=f"sums{h}") for h in halves}
+            for h in halves:
+                nc.scalar.copy(out=sums[h][:], in_=turned[h][:])
+            for h in halves:
+                back = psum.tile([P, 256], F32, name="acc")
+                for u in (0, P):
+                    nc.tensor.transpose(back[:, u : u + P], sums[h][:, u : u + P], identity[:])
+                result = held.tile([P, 256], F32, name=f"result{h}")
+                nc.scalar.copy(out=result[:], in_=back[:])
+                nc.scalar.dma_start(out=out[:, h : h + 256], in_=result[:])
 
         def finish(t0, t1):
             u = slice(t0 - ON_VECTOR, t1 - ON_VECTOR)

@@ -39,7 +39,7 @@ def tile_moe_tk_lin_silu_kernel(
 
         planes = held.tile([P, 2 * T], U8, name="planes", align_bytes=64)
         codes = [
-            held.tile([P, 2 * T if a < PASSES - 1 else T], U32, name=f"codes{a}", align_bytes=64) for a in range(PASSES)
+            held.tile([P, (2 * T, 4 * T, T)[a]], U32, name=f"codes{a}", align_bytes=64) for a in range(PASSES)
         ]
         low = held.tile([P, S], U8, name="low", align_bytes=64)
         ws8 = held.tile([P, E, N], U8, name="ws8", align_bytes=64)
@@ -56,10 +56,10 @@ def tile_moe_tk_lin_silu_kernel(
         identity = held.tile([P, P], F32, name="identity")
         make_identity(nc, identity[:])
 
-        chunks = [(0, 0, 512), (0, 512, 256), (0, 768, 256)] + [(a, t0, 512) for a in (1, 2) for t0 in (0, 512)]
+        chunks = [(a, t0, n) for a in (0, 1) for t0, n in ((0, 512), (512, 256), (768, 256))] + [(2, 0, 512), (2, 512, 512)]
         raw = {}
         for a, t0, n in chunks:
-            r = held.tile([P, 4, n], F32, name=f"raw{a}_{t0}")
+            r = held.tile([P, 4, n], F32, name=f"raw{a}_{t0}", tag=f"raw{a}_{t0}", align_bytes=64)
             nc.sync.dma_start(
                 out=r[:], in_=xT[512 * a : 512 * a + 512, t0 : t0 + n].rearrange("(p j) t -> p j t", j=4)
             )
@@ -84,17 +84,26 @@ def tile_moe_tk_lin_silu_kernel(
         for r, pos in enumerate((pos1, pos2, pos3)):
             nc.sync.dma_start(pos_t[r][:], pos)
 
-        HELD_BACK = 2304
-        slot_codes = [
-            held.tile([P, HELD_BACK if a == 1 else S], U32, name=f"slot_codes{a}", align_bytes=64) for a in range(PASSES)
-        ]
+        HELD_BACK = (2816, 2048, S)
+        slot_codes = [held.tile([P, HELD_BACK[a]], U32, name=f"slot_codes{a}", align_bytes=64) for a in range(PASSES)]
         slot_planes = held.tile([P, S], U8, name="slot_planes", align_bytes=64)
+        late_codes = {}
+
+        def words_of(a, s0, s1):
+            width = T if s1 - s0 <= 768 else 2 * T if s1 - s0 <= 1536 else 4 * T
+            return codes[a][:, 0:width].indirect(offs_t[:, s0 // 16 : s1 // 16])
 
         def gather_codes(a, s0, s1):
-            nc.vector.tensor_copy(out=slot_codes[a][:, s0:s1], in_=codes[a][:].indirect(offs_t[:, s0 // 16 : s1 // 16]))
+            nc.vector.tensor_copy(out=slot_codes[a][:, s0:s1], in_=words_of(a, s0, s1))
+
+        def gather_late_codes(a, s0, s1, tag):
+            late = held.tile([P, s1 - s0], U32, name=f"late_codes{a}_{s0}", tag=tag, align_bytes=64)
+            nc.vector.tensor_copy(out=late[:], in_=words_of(a, s0, s1))
+            for s in range(s0, s1, 128):
+                late_codes[a, s] = late[:, s - s0 : s - s0 + 128]
 
         def round_and_quantise(a, t0, n, on_scalar):
-            grouped = held.tile([P, n, 4], BF16, name=f"grouped{a}_{t0}", tag={(2, 0): "late", (2, 512): "later"}.get((a, t0), f"grouped{a}_{t0}"), align_bytes=64)
+            grouped = held.tile([P, n, 4], BF16, name=f"grouped{a}_{t0}", tag=f"grouped{a}_{t0}", align_bytes=64)
             v = n - on_scalar
             if on_scalar:
                 nc.scalar.activation(
@@ -119,15 +128,26 @@ def tile_moe_tk_lin_silu_kernel(
         round_and_quantise(0, 512, 256, 128)
         round_and_quantise(0, 768, 256, 128)
         gather_codes(0, 0, 1536)
-        gather_codes(0, 1536, 2688)
+        gather_codes(0, 1536, 2816)
         round_and_quantise(1, 0, 512, 512)
-        round_and_quantise(1, 512, 512, 512)
-        gather_codes(0, 2688, 3072)
-        gather_codes(1, 0, 1536)
-        gather_codes(1, 1536, 2304)
+        grouped = held.tile([P, 512, 4], BF16, name="grouped1_512", align_bytes=64)
+        for t0 in (512, 768):
+            nc.scalar.activation(
+                out=grouped[:, t0 - 512 : t0 - 256, :].rearrange("p (c i) j -> p c j i", i=4),
+                in_=raw[1, t0][:].rearrange("p j (c i) -> p c j i", i=4),
+                func=COPY,
+            )
+        nc.vector.quantize_mx(
+            out=codes[1][:, 512:T].bitcast(FP8X4),
+            scales=planes[:, 512:T],
+            in_=grouped[:].rearrange("p t j -> p (t j)"),
+        )
+        gather_late_codes(0, 2816, S, "raw1_768")
+        gather_codes(1, 0, 2048)
         round_and_quantise(2, 0, 512, 512)
         round_and_quantise(2, 512, 512, 512)
-        gates = held.tile([P, TOP, T], F32, name="gates", tag="late", align_bytes=64)
+        gather_late_codes(1, 2048, 2304, "raw2_512")
+        gates = held.tile([P, TOP, T], F32, name="gates", tag="grouped2_0", align_bytes=64)
         nc.scalar.dma_start(out=gates[:], in_=gate.rearrange("r p t -> p r t"))
 
         def gather_bytes(s0, s1):
@@ -144,8 +164,7 @@ def tile_moe_tk_lin_silu_kernel(
         gather_codes(2, 768, 1536)
         gather_bytes(2304, 3072)
         gather_codes(2, 1536, 2304)
-        late_codes = held.tile([P, S - HELD_BACK], U32, name="late_codes", tag="later", align_bytes=64)
-        nc.vector.tensor_copy(out=late_codes[:], in_=codes[1][:].indirect(offs_t[:, HELD_BACK // 16 : S // 16]))
+        gather_late_codes(1, 2304, S, "grouped2_512")
         gather_codes(2, 2304, 2816)
         gather_codes(2, 2816, 2944)
         gather_codes(2, 2944, 3072)
@@ -166,8 +185,8 @@ def tile_moe_tk_lin_silu_kernel(
                     lhsT=lhsT,
                     lhsT_scale=lhsT_scale,
                     rhs=(
-                        late_codes[:, s0 - HELD_BACK : s0 - HELD_BACK + 128]
-                        if a == 1 and s0 >= HELD_BACK
+                        late_codes[a, s0]
+                        if s0 >= HELD_BACK[a]
                         else slot_codes[a][:, cols]
                     ).bitcast(FP8X4),
                     rhs_scale=low[:, cols] if a == 2 else slot_planes[PLANE[a] : P, cols],

@@ -56,7 +56,7 @@ def tile_moe_tk_lin_silu_kernel(
         identity = held.tile([P, P], F32, name="identity")
         make_identity(nc, identity[:])
 
-        chunks = [(a, t0, n) for a in (0, 1) for t0, n in ((0, 512), (512, 256), (768, 256))] + [(2, 0, 512), (2, 512, 512)]
+        chunks = [(0, 0, 512), (0, 512, 384), (0, 896, 128), (1, 0, 512), (1, 512, 256), (1, 768, 256), (2, 0, 512), (2, 512, 512)]
         raw = {}
         for a, t0, n in chunks:
             r = held.tile([P, 4, n], F32, name=f"raw{a}_{t0}", tag=f"raw{a}_{t0}", align_bytes=64)
@@ -64,7 +64,7 @@ def tile_moe_tk_lin_silu_kernel(
                 out=r[:], in_=xT[512 * a : 512 * a + 512, t0 : t0 + n].rearrange("(p j) t -> p j t", j=4)
             )
             raw[a, t0] = r
-            if a == 0 and t0 == 768:
+            if a == 0 and t0 == 896:
                 nc.sync.dma_start(offs_t[:], offs)
         for q in range(4):
             nc.sync.dma_start(
@@ -125,8 +125,8 @@ def tile_moe_tk_lin_silu_kernel(
                     )
 
         round_and_quantise(0, 0, 512, 256)
-        round_and_quantise(0, 512, 256, 128)
-        round_and_quantise(0, 768, 256, 128)
+        round_and_quantise(0, 512, 384, 128)
+        round_and_quantise(0, 896, 128, 0)
         gather_codes(0, 0, 1536)
         gather_codes(0, 1536, 2816)
         round_and_quantise(1, 0, 512, 512)

@@ -22,8 +22,21 @@ COPY = mybir.ActivationFunctionType.Copy
 SILU = mybir.ActivationFunctionType.Silu
 MULT = mybir.AluOpType.mult
 
-CUT = 1536
-PLANE = (4, 0, 8)
+FIRST_ROW = (4, 0, 8)
+
+PIECES = (
+    ((512, 256), (384, 128), (128, 0)),
+    ((512, 512), (256, 256), (256, 256)),
+    ((512, 512), (512, 512)),
+)
+QUANTISE_WIDTHS = (512, 256, 128)
+
+GROUP = 128
+SPACER = 256
+EARLY = (S - SPACER, 2048, S)
+QUARTER = S // 4
+ON_TENSOR = 512
+HALF = 256
 
 
 def tile_moe_tk_lin_silu_kernel(
@@ -38,41 +51,37 @@ def tile_moe_tk_lin_silu_kernel(
         pos_t = [held.tile([P, T // 16], U16, name=f"pos_t{r}") for r in range(TOP)]
 
         planes = held.tile([P, 2 * T], U8, name="planes", align_bytes=64)
-        codes = [
-            held.tile([P, (2 * T, 4 * T, T)[a]], U32, name=f"codes{a}", align_bytes=64) for a in range(PASSES)
-        ]
-        low = held.tile([P, S], U8, name="low", align_bytes=64)
-        ws8 = held.tile([P, E, N], U8, name="ws8", align_bytes=64)
-        ws4 = held.tile([P, 2 * E, N], U8, name="ws4", align_bytes=64)
-        warm = held.tile([P, 1], F32, name="warm")
-        nc.vector.memset(warm[:], 0.0)
-        nc.vector.memset(planes[:].bitcast(I32), 0)
-        nc.vector.memset(ws8[:].rearrange("p e n -> p (e n)").bitcast(I32), 0)
-        nc.vector.memset(ws4[:].rearrange("p e n -> p (e n)").bitcast(I32), 0)
-        nc.vector.memset(low[:].bitcast(I32), 0)
-        warm_out = held.tile([P, 1], F32, name="warm_out")
-        nc.scalar.activation(out=warm_out[:], in_=warm[:], func=SILU)
+        codes = [held.tile([P, (2 * T, 4 * T, T)[a]], U32, name=f"codes{a}", align_bytes=64) for a in range(PASSES)]
+        moved_plane = held.tile([P, S], U8, name="moved_plane", align_bytes=64)
+        w8_plane = held.tile([P, E, N], U8, name="w8_plane", align_bytes=64)
+        w4_plane = held.tile([P, 2 * E, N], U8, name="w4_plane", align_bytes=64)
+        nc.vector.memset(planes[:, 0:T].bitcast(I32), 0)
+        nc.vector.memset(w8_plane[:].rearrange("p e n -> p (e n)").bitcast(I32), 0)
+        nc.vector.memset(w4_plane[:].rearrange("p e n -> p (e n)").bitcast(I32), 0)
+        nc.vector.memset(moved_plane[:].bitcast(I32), 0)
 
         identity = held.tile([P, P], F32, name="identity")
         make_identity(nc, identity[:])
 
-        chunks = [(0, 0, 512), (0, 512, 384), (0, 896, 128), (1, 0, 512), (1, 512, 256), (1, 768, 256), (2, 0, 512), (2, 512, 512)]
         raw = {}
-        for a, t0, n in chunks:
-            r = held.tile([P, 4, n], F32, name=f"raw{a}_{t0}", tag=f"raw{a}_{t0}", align_bytes=64)
-            nc.sync.dma_start(
-                out=r[:], in_=xT[512 * a : 512 * a + 512, t0 : t0 + n].rearrange("(p j) t -> p j t", j=4)
-            )
-            raw[a, t0] = r
-            if a == 0 and t0 == 896:
+        for a in range(PASSES):
+            t0 = 0
+            for n, on_scalar in PIECES[a]:
+                piece = held.tile([P, 4, n], F32, name=f"raw{a}_{t0}", tag=f"raw{a}_{t0}", align_bytes=64)
+                nc.sync.dma_start(
+                    out=piece[:], in_=xT[512 * a : 512 * a + 512, t0 : t0 + n].rearrange("(p j) t -> p j t", j=4)
+                )
+                raw[a, t0] = (piece, n, on_scalar)
+                t0 = t0 + n
+            if a == 0:
                 nc.sync.dma_start(offs_t[:], offs)
         for q in range(4):
             nc.sync.dma_start(
-                out=ws8[32 * q : 32 * q + 4, :, :].bitcast(I32),
+                out=w8_plane[32 * q : 32 * q + 4, :, :].bitcast(I32),
                 in_=w8_scales[:, 0, 4 * q : 4 * q + 4, :].rearrange("e q n -> q e n").bitcast(I32),
             )
             nc.sync.dma_start(
-                out=ws4[32 * q : 32 * q + 4, :, :].bitcast(I32),
+                out=w4_plane[32 * q : 32 * q + 4, :, :].bitcast(I32),
                 in_=w4_scales[:, :, 4 * q : 4 * q + 4, :].rearrange("e a q n -> q (e a) n").bitcast(I32),
             )
         w8 = held.tile([P, E, 4 * N], U8, name="w8", align_bytes=64)
@@ -84,163 +93,145 @@ def tile_moe_tk_lin_silu_kernel(
         for r, pos in enumerate((pos1, pos2, pos3)):
             nc.sync.dma_start(pos_t[r][:], pos)
 
-        HELD_BACK = (2816, 2048, S)
-        slot_codes = [held.tile([P, HELD_BACK[a]], U32, name=f"slot_codes{a}", align_bytes=64) for a in range(PASSES)]
+        slot_codes = [held.tile([P, EARLY[a]], U32, name=f"slot_codes{a}", align_bytes=64) for a in range(PASSES)]
         slot_planes = held.tile([P, S], U8, name="slot_planes", align_bytes=64)
-        late_codes = {}
+        held_back = {}
+
+        def round_and_quantise(a):
+            for t0 in sorted(t for pass_, t in raw if pass_ == a):
+                piece, n, on_scalar = raw[a, t0]
+                rounded = held.tile([P, n, 4], BF16, name=f"rounded{a}_{t0}", tag=f"rounded{a}_{t0}", align_bytes=64)
+                on_vector = n - on_scalar
+                if on_scalar:
+                    nc.scalar.activation(
+                        out=rounded[:, on_vector:n, :].rearrange("p (c i) j -> p c j i", i=4),
+                        in_=piece[:, :, on_vector:n].rearrange("p j (c i) -> p c j i", i=4),
+                        func=COPY,
+                    )
+                if on_vector:
+                    nc.vector.tensor_copy(
+                        out=rounded[:, 0:on_vector, :].rearrange("p (c i) j -> p c j i", i=4),
+                        in_=piece[:, :, 0:on_vector].rearrange("p j (c i) -> p c j i", i=4),
+                    )
+                u0 = 0
+                for share_end in (on_vector, n):
+                    for width in QUANTISE_WIDTHS:
+                        if u0 + width <= share_end:
+                            nc.vector.quantize_mx(
+                                out=codes[a][:, t0 + u0 : t0 + u0 + width].bitcast(FP8X4),
+                                scales=planes[FIRST_ROW[a] : P, t0 + u0 : t0 + u0 + width],
+                                in_=rounded[:, u0 : u0 + width, :].rearrange("p t j -> p (t j)"),
+                            )
+                            u0 = u0 + width
 
         def words_of(a, s0, s1):
-            width = T if s1 - s0 <= 768 else 2 * T if s1 - s0 <= 1536 else 4 * T
+            width = min(w for w in (T, 2 * T, 4 * T) if 4 * (s1 - s0) <= 3 * w)
             return codes[a][:, 0:width].indirect(offs_t[:, s0 // 16 : s1 // 16])
 
-        def gather_codes(a, s0, s1):
+        def gather_words(a, s0, s1):
             nc.vector.tensor_copy(out=slot_codes[a][:, s0:s1], in_=words_of(a, s0, s1))
 
-        def gather_late_codes(a, s0, s1, tag):
-            late = held.tile([P, s1 - s0], U32, name=f"late_codes{a}_{s0}", tag=tag, align_bytes=64)
+        def gather_held_back_words(a, s0, s1, tag):
+            late = held.tile([P, s1 - s0], U32, name=f"held_back{a}_{s0}", tag=tag, align_bytes=64)
             nc.vector.tensor_copy(out=late[:], in_=words_of(a, s0, s1))
-            for s in range(s0, s1, 128):
-                late_codes[a, s] = late[:, s - s0 : s - s0 + 128]
+            for s in range(s0, s1, GROUP):
+                held_back[a, s] = late[:, s - s0 : s - s0 + GROUP]
 
-        def round_and_quantise(a, t0, n, on_scalar):
-            grouped = held.tile([P, n, 4], BF16, name=f"grouped{a}_{t0}", tag=f"grouped{a}_{t0}", align_bytes=64)
-            v = n - on_scalar
-            if on_scalar:
-                nc.scalar.activation(
-                    out=grouped[:, v:n, :].rearrange("p (c i) j -> p c j i", i=4),
-                    in_=raw[a, t0][:, :, v:n].rearrange("p j (c i) -> p c j i", i=4),
-                    func=COPY,
-                )
-            if v:
-                nc.vector.tensor_copy(
-                    out=grouped[:, 0:v, :].rearrange("p (c i) j -> p c j i", i=4),
-                    in_=raw[a, t0][:, :, 0:v].rearrange("p j (c i) -> p c j i", i=4),
-                )
-            for u0, u1 in ((0, v), (v, n)):
-                if u0 < u1:
-                    nc.vector.quantize_mx(
-                        out=codes[a][:, t0 + u0 : t0 + u1].bitcast(FP8X4),
-                        scales=planes[PLANE[a] : P, t0 + u0 : t0 + u1],
-                        in_=grouped[:, u0:u1, :].rearrange("p t j -> p (t j)"),
-                    )
-
-        round_and_quantise(0, 0, 512, 256)
-        round_and_quantise(0, 512, 384, 128)
-        round_and_quantise(0, 896, 128, 0)
-        gather_codes(0, 0, 1536)
-        gather_codes(0, 1536, 2816)
-        round_and_quantise(1, 0, 512, 512)
-        grouped = held.tile([P, 512, 4], BF16, name="grouped1_512", align_bytes=64)
-        for t0 in (512, 768):
-            nc.scalar.activation(
-                out=grouped[:, t0 - 512 : t0 - 256, :].rearrange("p (c i) j -> p c j i", i=4),
-                in_=raw[1, t0][:].rearrange("p j (c i) -> p c j i", i=4),
-                func=COPY,
-            )
-        nc.vector.quantize_mx(
-            out=codes[1][:, 512:T].bitcast(FP8X4),
-            scales=planes[:, 512:T],
-            in_=grouped[:].rearrange("p t j -> p (t j)"),
-        )
-        gather_late_codes(0, 2816, S, "raw1_768")
-        gather_codes(1, 0, 2048)
-        round_and_quantise(2, 0, 512, 512)
-        round_and_quantise(2, 512, 512, 512)
-        gather_late_codes(1, 2048, 2304, "raw2_512")
-        gates = held.tile([P, TOP, T], F32, name="gates", tag="grouped2_0", align_bytes=64)
-        nc.scalar.dma_start(out=gates[:], in_=gate.rearrange("r p t -> p r t"))
-
-        def gather_bytes(s0, s1):
+        def gather_scale_bytes(s0, s1):
             nc.vector.tensor_copy(out=slot_planes[:, s0:s1], in_=planes[:].indirect(offs_t[:, s0 // 16 : s1 // 16]))
             for q in range(4):
+                row = 32 * q + FIRST_ROW[2]
                 nc.sync.dma_start(
-                    out=low[32 * q : 32 * q + 4, s0:s1].bitcast(I32),
-                    in_=slot_planes[32 * q + 8 : 32 * q + 12, s0:s1].bitcast(I32),
+                    out=moved_plane[32 * q : 32 * q + 4, s0:s1].bitcast(I32),
+                    in_=slot_planes[row : row + 4, s0:s1].bitcast(I32),
                 )
 
-        gather_bytes(0, 768)
-        gather_codes(2, 0, 768)
-        gather_bytes(768, 2304)
-        gather_codes(2, 768, 1536)
-        gather_bytes(2304, 3072)
-        gather_codes(2, 1536, 2304)
-        gather_late_codes(1, 2304, S, "grouped2_512")
-        gather_codes(2, 2304, 2816)
-        gather_codes(2, 2816, 2944)
-        gather_codes(2, 2944, 3072)
+        round_and_quantise(0)
+        gather_words(0, 0, S // 2)
+        gather_words(0, S // 2, EARLY[0])
+        round_and_quantise(1)
+        gather_held_back_words(0, EARLY[0], S, "raw1_768")
+        gather_words(1, 0, EARLY[1])
+        round_and_quantise(2)
+        gather_held_back_words(1, EARLY[1], EARLY[1] + SPACER, "raw2_512")
+
+        gates = held.tile([P, TOP, T], F32, name="gates", tag="rounded2_0", align_bytes=64)
+        nc.scalar.dma_start(out=gates[:], in_=gate.rearrange("r p t -> p r t"))
+
+        gather_scale_bytes(0, QUARTER)
+        gather_words(2, 0, QUARTER)
+        gather_scale_bytes(QUARTER, 3 * QUARTER)
+        gather_words(2, QUARTER, 2 * QUARTER)
+        gather_scale_bytes(3 * QUARTER, S)
+        gather_words(2, 2 * QUARTER, 3 * QUARTER)
+        gather_held_back_words(1, 3 * QUARTER, S, "rounded2_512")
+        gather_words(2, 3 * QUARTER, S - 2 * GROUP)
+        gather_words(2, S - 2 * GROUP, S - GROUP)
+        gather_words(2, S - GROUP, S)
 
         y = held.tile([P, S], F32, name="y")
-        for s0 in range(0, S, 128):
+        for s0 in range(0, S, GROUP):
             e = s0 // C
-            cols = slice(s0, s0 + 128)
-            acc = psum.tile([P, 128], F32, name="acc")
+            cols = slice(s0, s0 + GROUP)
+            acc = psum.tile([P, GROUP], F32, name="bank")
             for a in range(PASSES):
                 if a == 0:
-                    lhsT, lhsT_scale = w8[:, e, :].bitcast(FP8X4), ws8[:, e, :]
+                    weights, weight_plane = w8[:, e, :].bitcast(FP8X4), w8_plane[:, e, :]
                 else:
                     m = 2 * e + a - 1
-                    lhsT, lhsT_scale = w4[:, m, :].bitcast(FP4X4), ws4[:, m, :]
+                    weights, weight_plane = w4[:, m, :].bitcast(FP4X4), w4_plane[:, m, :]
+                words = slot_codes[a][:, cols] if s0 < EARLY[a] else held_back[a, s0]
                 nc.tensor.matmul_mx(
                     out=acc[:],
-                    lhsT=lhsT,
-                    lhsT_scale=lhsT_scale,
-                    rhs=(
-                        late_codes[a, s0]
-                        if s0 >= HELD_BACK[a]
-                        else slot_codes[a][:, cols]
-                    ).bitcast(FP8X4),
-                    rhs_scale=low[:, cols] if a == 2 else slot_planes[PLANE[a] : P, cols],
+                    lhsT=weights,
+                    lhsT_scale=weight_plane,
+                    rhs=words.bitcast(FP8X4),
+                    rhs_scale=moved_plane[:, cols] if a == 2 else slot_planes[FIRST_ROW[a] : P, cols],
                     start=(a == 0),
                     stop=(a == PASSES - 1),
                 )
             nc.scalar.activation(out=y[:, cols], in_=acc[:], func=SILU, bias=bias[:, e : e + 1])
 
         parts = [held.tile([P, T], F32, name=f"part{r}") for r in range(TOP)]
-        ON_VECTOR = 512
-        total = held.tile([P, T - ON_VECTOR], F32, name="total")
-        last = held.tile([P, T - ON_VECTOR], F32, name="last")
+        first_two = held.tile([P, T - ON_TENSOR], F32, name="first_two")
+        all_three = held.tile([P, T - ON_TENSOR], F32, name="all_three")
 
         def fetch(r, t0, t1):
             nc.vector.tensor_tensor(
                 parts[r][:, t0:t1], y[:].indirect(pos_t[r][:, t0 // 16 : t1 // 16]), gates[:, r, t0:t1], MULT
             )
 
-        def combine_on_tensor(t0, t1):
-            halves = range(t0, t1, 256)
-            turned = {h: psum.tile([P, 256], F32, name="acc") for h in halves}
-            for r in range(TOP):
-                fetch(r, t0, t1)
-                for h in halves:
-                    for u in (0, P):
-                        nc.tensor.matmul(
-                            turned[h][:, u : u + P],
-                            lhsT=parts[r][:, h + u : h + u + P],
-                            rhs=identity[:],
-                            is_transpose=True,
-                            start=(r == 0 and u == 0),
-                            stop=(r == TOP - 1 and u == P),
-                        )
-            sums = {h: held.tile([P, 256], F32, name=f"sums{h}") for h in halves}
+        halves = range(0, ON_TENSOR, HALF)
+        turned = {h: psum.tile([P, HALF], F32, name="bank") for h in halves}
+        for r in range(TOP):
+            fetch(r, 0, ON_TENSOR)
             for h in halves:
-                nc.scalar.copy(out=sums[h][:], in_=turned[h][:])
-            for h in halves:
-                back = psum.tile([P, 256], F32, name="acc")
-                for u in (0, P):
-                    nc.tensor.transpose(back[:, u : u + P], sums[h][:, u : u + P], identity[:])
-                result = held.tile([P, 256], F32, name=f"result{h}")
-                nc.scalar.copy(out=result[:], in_=back[:])
-                nc.scalar.dma_start(out=out[:, h : h + 256], in_=result[:])
+                for u in range(0, HALF, P):
+                    nc.tensor.matmul(
+                        turned[h][:, u : u + P],
+                        lhsT=parts[r][:, h + u : h + u + P],
+                        rhs=identity[:],
+                        is_transpose=True,
+                        start=(r == 0 and u == 0),
+                        stop=(r == TOP - 1 and u == HALF - P),
+                    )
+        sums = {h: held.tile([P, HALF], F32, name=f"sums{h}") for h in halves}
+        for h in halves:
+            nc.scalar.copy(out=sums[h][:], in_=turned[h][:])
+        for h in halves:
+            back = psum.tile([P, HALF], F32, name="bank")
+            for u in range(0, HALF, P):
+                nc.tensor.transpose(back[:, u : u + P], sums[h][:, u : u + P], identity[:])
+            result = held.tile([P, HALF], F32, name=f"result{h}")
+            nc.scalar.copy(out=result[:], in_=back[:])
+            nc.scalar.dma_start(out=out[:, h : h + HALF], in_=result[:])
 
-        def finish(t0, t1):
-            u = slice(t0 - ON_VECTOR, t1 - ON_VECTOR)
-            nc.vector.tensor_add(last[:, u], total[:, u], parts[2][:, t0:t1])
-            nc.sync.dma_start(out=out[:, t0:t1], in_=last[:, u])
-
-        combine_on_tensor(0, ON_VECTOR)
-        fetch(0, ON_VECTOR, T)
-        fetch(1, ON_VECTOR, T)
-        fetch(2, ON_VECTOR, 768)
-        nc.vector.tensor_add(total[:], parts[0][:, ON_VECTOR:T], parts[1][:, ON_VECTOR:T])
-        fetch(2, 768, T)
-        finish(ON_VECTOR, 768)
-        finish(768, T)
+        fetch(0, ON_TENSOR, T)
+        fetch(1, ON_TENSOR, T)
+        fetch(2, ON_TENSOR, T - HALF)
+        nc.vector.tensor_add(first_two[:], parts[0][:, ON_TENSOR:T], parts[1][:, ON_TENSOR:T])
+        fetch(2, T - HALF, T)
+        for t0 in range(ON_TENSOR, T, HALF):
+            u = slice(t0 - ON_TENSOR, t0 - ON_TENSOR + HALF)
+            nc.vector.tensor_add(all_three[:, u], first_two[:, u], parts[2][:, t0 : t0 + HALF])
+            nc.sync.dma_start(out=out[:, t0 : t0 + HALF], in_=all_three[:, u])

@@ -55,10 +55,15 @@ def tile_moe_tk_lin_silu_kernel(
         moved_plane = held.tile([P, S], U8, name="moved_plane", align_bytes=64)
         w8_plane = held.tile([P, E, N], U8, name="w8_plane", align_bytes=64)
         w4_plane = held.tile([P, 2 * E, N], U8, name="w4_plane", align_bytes=64)
+        warm_in = held.tile([P, 1], F32, name="warm_in")
+        nc.vector.memset(warm_in[:], 0.0)
         nc.vector.memset(planes[:, 0:T].bitcast(I32), 0)
         nc.vector.memset(w8_plane[:].rearrange("p e n -> p (e n)").bitcast(I32), 0)
         nc.vector.memset(w4_plane[:].rearrange("p e n -> p (e n)").bitcast(I32), 0)
         nc.vector.memset(moved_plane[:].bitcast(I32), 0)
+
+        warm_out = held.tile([P, 1], F32, name="warm_out")
+        nc.scalar.activation(out=warm_out[:], in_=warm_in[:], func=SILU)
 
         identity = held.tile([P, P], F32, name="identity")
         make_identity(nc, identity[:])

@@ -25,7 +25,7 @@ MULT = mybir.AluOpType.mult
 FIRST_ROW = (4, 0, 8)
 
 PIECES = (
-    ((512, 256), (384, 128), (128, 0)),
+    ((512, 256), (256, 128), (128, 128), (128, 0)),
     ((512, 512), (256, 256), (256, 256)),
     ((512, 512), (512, 512)),
 )
@@ -223,13 +223,13 @@ def tile_moe_tk_lin_silu_kernel(
         sums = {h: held.tile([P, HALF], F32, name=f"sums{h}") for h in halves}
         for h in halves:
             nc.scalar.copy(out=sums[h][:], in_=turned[h][:])
+        result = held.tile([P, ON_TENSOR], F32, name="result")
         for h in halves:
             back = psum.tile([P, HALF], F32, name="bank")
             for u in range(0, HALF, P):
                 nc.tensor.transpose(back[:, u : u + P], sums[h][:, u : u + P], identity[:])
-            result = held.tile([P, HALF], F32, name=f"result{h}")
-            nc.scalar.copy(out=result[:], in_=back[:])
-            nc.scalar.dma_start(out=out[:, h : h + HALF], in_=result[:])
+            nc.scalar.copy(out=result[:, h : h + HALF], in_=back[:])
+        nc.scalar.dma_start(out=out[:, 0:ON_TENSOR], in_=result[:])
 
         fetch(0, ON_TENSOR, T)
         fetch(1, ON_TENSOR, T)

@@ -209,8 +209,11 @@ def tile_moe_tk_lin_silu_kernel(
         halves = range(0, ON_TENSOR, HALF)
         turned = {h: psum.tile([P, HALF], F32, name="bank") for h in halves}
         for r in range(TOP):
-            fetch(r, 0, ON_TENSOR)
+            if r < TOP - 1:
+                fetch(r, 0, ON_TENSOR)
             for h in halves:
+                if r == TOP - 1:
+                    fetch(r, h, h + HALF)
                 for u in range(0, HALF, P):
                     nc.tensor.matmul(
                         turned[h][:, u : u + P],

@@ -197,49 +197,101 @@ def tile_moe_tk_lin_silu_kernel(
                 )
             nc.scalar.activation(out=y[:, cols], in_=acc[:], func=SILU, bias=bias[:, e : e + 1])
 
-        parts = [held.tile([P, T], F32, name=f"part{r}") for r in range(TOP)]
-        first_two = held.tile([P, T - ON_TENSOR], F32, name="first_two")
-        all_three = held.tile([P, T - ON_TENSOR], F32, name="all_three")
+        part = {}
+        plain = {}
 
-        def fetch(r, t0, t1):
-            nc.vector.tensor_tensor(
-                parts[r][:, t0:t1], y[:].indirect(pos_t[r][:, t0 // 16 : t1 // 16]), gates[:, r, t0:t1], MULT
-            )
+        def results_of(r, t0, t1):
+            return y[:].indirect(pos_t[r][:, t0 // 16 : t1 // 16])
 
-        halves = range(0, ON_TENSOR, HALF)
-        turned = {h: psum.tile([P, HALF], F32, name="bank") for h in halves}
-        for r in range(TOP):
-            if r < TOP - 1:
-                fetch(r, 0, ON_TENSOR)
-            for h in halves:
-                if r == TOP - 1:
-                    fetch(r, h, h + HALF)
-                for u in range(0, HALF, P):
-                    nc.tensor.matmul(
-                        turned[h][:, u : u + P],
-                        lhsT=parts[r][:, h + u : h + u + P],
-                        rhs=identity[:],
-                        is_transpose=True,
-                        start=(r == 0 and u == 0),
-                        stop=(r == TOP - 1 and u == HALF - P),
-                    )
-        sums = {h: held.tile([P, HALF], F32, name=f"sums{h}") for h in halves}
-        for h in halves:
-            nc.scalar.copy(out=sums[h][:], in_=turned[h][:])
-        result = held.tile([P, ON_TENSOR], F32, name="result")
-        for h in halves:
-            back = psum.tile([P, HALF], F32, name="bank")
-            for u in range(0, HALF, P):
-                nc.tensor.transpose(back[:, u : u + P], sums[h][:, u : u + P], identity[:])
-            nc.scalar.copy(out=result[:, h : h + HALF], in_=back[:])
-        nc.scalar.dma_start(out=out[:, 0:ON_TENSOR], in_=result[:])
+        def new_part(r, t0, t1):
+            tile = held.tile([P, t1 - t0], F32, name=f"part{r}_{t0}", tag=f"part{r}_{t0}")
+            for t in range(t0, t1, P):
+                part[r, t] = (tile, t - t0)
+            return tile
 
-        fetch(0, ON_TENSOR, T)
-        fetch(1, ON_TENSOR, T)
-        fetch(2, ON_TENSOR, T - HALF)
-        nc.vector.tensor_add(first_two[:], parts[0][:, ON_TENSOR:T], parts[1][:, ON_TENSOR:T])
-        fetch(2, T - HALF, T)
-        for t0 in range(ON_TENSOR, T, HALF):
-            u = slice(t0 - ON_TENSOR, t0 - ON_TENSOR + HALF)
-            nc.vector.tensor_add(all_three[:, u], first_two[:, u], parts[2][:, t0 : t0 + HALF])
-            nc.sync.dma_start(out=out[:, t0 : t0 + HALF], in_=all_three[:, u])
+        def part_of(r, t0, t1):
+            tile, u = part[r, t0]
+            return tile[:, u : u + t1 - t0]
+
+        def fetch_gated(r, t0, t1):
+            nc.vector.tensor_tensor(new_part(r, t0, t1)[:], results_of(r, t0, t1), gates[:, r, t0:t1], MULT)
+
+        def fetch_plain(r, t0, t1, tag=None):
+            tile = held.tile([P, t1 - t0], F32, name=f"plain{r}_{t0}", tag=tag or f"plain{r}_{t0}")
+            for t in range(t0, t1, P):
+                plain[r, t] = (tile, t - t0)
+            nc.scalar.activation(out=tile[:], in_=results_of(r, t0, t1), func=COPY)
+
+        def apply_gate(r, t0, t1):
+            tile, u = plain[r, t0]
+            nc.vector.tensor_tensor(new_part(r, t0, t1)[:], tile[:, u : u + t1 - t0], gates[:, r, t0:t1], MULT)
+
+        turned = {}
+        sums = {}
+        result = held.tile([P, T], F32, name="result")
+        first_two = held.tile([P, T], F32, name="first_two")
+
+        def turn(r, t0, t1, first=False, last=False):
+            if first:
+                turned[t0] = psum.tile([P, t1 - t0], F32, name="bank")
+            for t in range(t0, t1, P):
+                nc.tensor.matmul(
+                    turned[t0][:, t - t0 : t - t0 + P],
+                    lhsT=part_of(r, t, t + P),
+                    rhs=identity[:],
+                    is_transpose=True,
+                    start=(first and t == t0),
+                    stop=(last and t == t1 - P),
+                )
+
+        def copy_sums(t0, t1):
+            sums[t0] = held.tile([P, t1 - t0], F32, name=f"sums{t0}")
+            nc.scalar.copy(out=sums[t0][:], in_=turned[t0][:])
+
+        def turn_back(t0, t1):
+            back = psum.tile([P, t1 - t0], F32, name="bank")
+            for u in range(0, t1 - t0, P):
+                nc.tensor.transpose(back[:, u : u + P], sums[t0][:, u : u + P], identity[:])
+            nc.scalar.copy(out=result[:, t0:t1], in_=back[:])
+
+        def add_two(r0, r1, t0, t1):
+            nc.vector.tensor_add(first_two[:, t0:t1], part_of(r0, t0, t1), part_of(r1, t0, t1))
+
+        def add_third(r, t0, t1):
+            nc.vector.tensor_add(result[:, t0:t1], first_two[:, t0:t1], part_of(r, t0, t1))
+
+        def store(queue, t0, t1):
+            queue.dma_start(out=out[:, t0:t1], in_=result[:, t0:t1])
+
+        q0, q1, q2, q3, q4 = range(0, T + 1, HALF)
+        fetch_plain(1, q0, q2)
+        fetch_gated(0, q0, q2)
+        fetch_gated(2, q0, q1)
+        apply_gate(1, q0, q2)
+        fetch_gated(2, q1, q2)
+        fetch_gated(0, q2, q3)
+        turn(0, q0, q1, first=True)
+        turn(0, q1, q2, first=True)
+        turn(2, q0, q1)
+        turn(1, q0, q1, last=True)
+        turn(1, q1, q2)
+        turn(2, q1, q2, last=True)
+        fetch_plain(1, q2, q4)
+        fetch_plain(2, q2, q3)
+        fetch_plain(0, q3, q4)
+        copy_sums(q0, q1)
+        copy_sums(q1, q2)
+        fetch_plain(2, q3, q4, tag=f"part2_{q1}")
+        turn_back(q0, q1)
+        turn_back(q1, q2)
+        store(nc.scalar, q0, q2)
+        apply_gate(1, q2, q4)
+        apply_gate(2, q2, q3)
+        add_two(0, 1, q2, q3)
+        apply_gate(0, q3, q4)
+        add_third(2, q2, q3)
+        store(nc.sync, q2, q3)
+        apply_gate(2, q3, q4)
+        add_two(0, 1, q3, q4)
+        add_third(2, q3, q4)
+        store(nc.sync, q3, q4)

@@ -263,35 +263,34 @@ def tile_moe_tk_lin_silu_kernel(
         def store(queue, t0, t1):
             queue.dma_start(out=out[:, t0:t1], in_=result[:, t0:t1])
 
-        q0, q1, q2, q3, q4 = range(0, T + 1, HALF)
-        fetch_plain(1, q0, q2)
-        fetch_gated(0, q0, q2)
-        fetch_gated(2, q0, q1)
-        apply_gate(1, q0, q2)
-        fetch_gated(2, q1, q2)
-        fetch_gated(0, q2, q3)
-        turn(0, q0, q1, first=True)
-        turn(0, q1, q2, first=True)
-        turn(2, q0, q1)
-        turn(1, q0, q1, last=True)
-        turn(1, q1, q2)
-        turn(2, q1, q2, last=True)
-        fetch_plain(1, q2, q4)
-        fetch_plain(2, q2, q3)
-        fetch_plain(0, q3, q4)
-        copy_sums(q0, q1)
-        copy_sums(q1, q2)
-        fetch_plain(2, q3, q4, tag=f"part2_{q1}")
-        turn_back(q0, q1)
-        turn_back(q1, q2)
-        store(nc.scalar, q0, q2)
-        apply_gate(1, q2, q4)
-        apply_gate(2, q2, q3)
-        add_two(0, 1, q2, q3)
-        apply_gate(0, q3, q4)
-        add_third(2, q2, q3)
-        store(nc.sync, q2, q3)
-        apply_gate(2, q3, q4)
-        add_two(0, 1, q3, q4)
-        add_third(2, q3, q4)
-        store(nc.sync, q3, q4)
+        b0, b1, b2, b3 = 384, 640, 896, T
+        fetch_plain(1, 0, b0)
+        fetch_gated(0, 0, b0)
+        fetch_gated(2, 0, b0)
+        apply_gate(1, 0, b0)
+        fetch_gated(0, b0, b1)
+        turn(0, 0, b0, first=True)
+        turn(2, 0, b0)
+        turn(1, 0, b0, last=True)
+        fetch_plain(1, b0, b1)
+        fetch_plain(2, b0, b1)
+        fetch_plain(0, b1, b3)
+        fetch_plain(1, b1, b3)
+        copy_sums(0, b0)
+        fetch_plain(2, b1, b3, tag="part1_0")
+        turn_back(0, b0)
+        store(nc.scalar, 0, b0)
+        apply_gate(1, b0, b1)
+        apply_gate(2, b0, b1)
+        apply_gate(0, b1, b3)
+        add_two(0, 1, b0, b1)
+        apply_gate(1, b1, b3)
+        add_third(2, b0, b1)
+        store(nc.sync, b0, b1)
+        add_two(0, 1, b1, b3)
+        apply_gate(2, b1, b2)
+        apply_gate(2, b2, b3)
+        add_third(2, b1, b2)
+        store(nc.sync, b1, b2)
+        add_third(2, b2, b3)
+        store(nc.sync, b2, b3)

@@ -205,7 +205,7 @@ def tile_moe_tk_lin_silu_kernel(
 
         def new_part(r, t0, t1):
             tile = held.tile([P, t1 - t0], F32, name=f"part{r}_{t0}", tag=f"part{r}_{t0}")
-            for t in range(t0, t1, P):
+            for t in range(t0, t1, 64):
                 part[r, t] = (tile, t - t0)
             return tile
 
@@ -218,7 +218,7 @@ def tile_moe_tk_lin_silu_kernel(
 
         def fetch_plain(r, t0, t1, tag=None):
             tile = held.tile([P, t1 - t0], F32, name=f"plain{r}_{t0}", tag=tag or f"plain{r}_{t0}")
-            for t in range(t0, t1, P):
+            for t in range(t0, t1, 64):
                 plain[r, t] = (tile, t - t0)
             nc.scalar.activation(out=tile[:], in_=results_of(r, t0, t1), func=COPY)
 
@@ -233,10 +233,10 @@ def tile_moe_tk_lin_silu_kernel(
 
         def turn(r, t0, t1, first=False, last=False):
             if first:
-                turned[t0] = psum.tile([P, t1 - t0], F32, name="bank")
+                turned[0] = psum.tile([P, t1 - t0], F32, name="bank")
             for t in range(t0, t1, P):
                 nc.tensor.matmul(
-                    turned[t0][:, t - t0 : t - t0 + P],
+                    turned[0][:, t : t + P],
                     lhsT=part_of(r, t, t + P),
                     rhs=identity[:],
                     is_transpose=True,
@@ -263,25 +263,32 @@ def tile_moe_tk_lin_silu_kernel(
         def store(queue, t0, t1):
             queue.dma_start(out=out[:, t0:t1], in_=result[:, t0:t1])
 
-        b0, b1, b2, b3 = 384, 640, 896, T
+        b0, b1, b2, b3 = 384, 640, 832, T
         fetch_plain(1, 0, b0)
-        fetch_gated(0, 0, b0)
-        fetch_gated(2, 0, b0)
+        fetch_gated(0, 0, P)
+        fetch_gated(0, P, b0)
         apply_gate(1, 0, b0)
+        fetch_gated(2, 0, b0)
         fetch_gated(0, b0, b1)
         turn(0, 0, b0, first=True)
-        turn(2, 0, b0)
-        turn(1, 0, b0, last=True)
-        fetch_plain(1, b0, b1)
-        fetch_plain(2, b0, b1)
+        turn(1, 0, b0)
+        turn(2, 0, b0, last=True)
+        pair = held.tile([P, 2, b1 - b0], F32, name="pair")
+        for r in (1, 2):
+            nc.scalar.activation(out=pair[:, r - 1, :], in_=results_of(r, b0, b1), func=COPY)
         fetch_plain(0, b1, b3)
         fetch_plain(1, b1, b3)
         copy_sums(0, b0)
-        fetch_plain(2, b1, b3, tag="part1_0")
+        late = held.tile([P, b3 - b1], F32, name="late", tag="part2_0")
+        for t0, t1 in ((b1, b2), (b2, b3)):
+            plain[2, t0] = (late, t0 - b1)
+            nc.scalar.activation(out=late[:, t0 - b1 : t1 - b1], in_=results_of(2, t0, t1), func=COPY)
         turn_back(0, b0)
         store(nc.scalar, 0, b0)
-        apply_gate(1, b0, b1)
-        apply_gate(2, b0, b1)
+        gated_pair = held.tile([P, 2 * (b1 - b0)], F32, name="gated_pair")
+        nc.vector.tensor_tensor(gated_pair[:].rearrange("p (r t) -> p r t", r=2), pair[:], gates[:, 1:3, b0:b1], MULT)
+        part[1, b0] = (gated_pair, 0)
+        part[2, b0] = (gated_pair, b1 - b0)
         apply_gate(0, b1, b3)
         add_two(0, 1, b0, b1)
         apply_gate(1, b1, b3)
@@ -291,6 +298,5 @@ def tile_moe_tk_lin_silu_kernel(
         apply_gate(2, b1, b2)
         apply_gate(2, b2, b3)
         add_third(2, b1, b2)
-        store(nc.sync, b1, b2)
         add_third(2, b2, b3)
-        store(nc.sync, b2, b3)
+        store(nc.sync, b1, b3)

@@ -263,40 +263,32 @@ def tile_moe_tk_lin_silu_kernel(
         def store(queue, t0, t1):
             queue.dma_start(out=out[:, t0:t1], in_=result[:, t0:t1])
 
-        b0, b1, b2, b3 = 384, 640, 832, T
+        b0, b1, b3 = 384, 768, T
         fetch_plain(1, 0, b0)
-        fetch_gated(0, 0, P)
-        fetch_gated(0, P, b0)
-        apply_gate(1, 0, b0)
+        fetch_gated(0, 0, b0)
         fetch_gated(2, 0, b0)
-        fetch_gated(0, b0, b1)
+        apply_gate(1, 0, b0)
+        fetch_gated(0, b0, b3)
         turn(0, 0, b0, first=True)
-        turn(1, 0, b0)
-        turn(2, 0, b0, last=True)
+        turn(2, 0, b0)
+        turn(1, 0, b0, last=True)
         pair = held.tile([P, 2, b1 - b0], F32, name="pair")
         for r in (1, 2):
             nc.scalar.activation(out=pair[:, r - 1, :], in_=results_of(r, b0, b1), func=COPY)
-        fetch_plain(0, b1, b3)
         fetch_plain(1, b1, b3)
         copy_sums(0, b0)
-        late = held.tile([P, b3 - b1], F32, name="late", tag="part2_0")
-        for t0, t1 in ((b1, b2), (b2, b3)):
-            plain[2, t0] = (late, t0 - b1)
-            nc.scalar.activation(out=late[:, t0 - b1 : t1 - b1], in_=results_of(2, t0, t1), func=COPY)
+        fetch_plain(2, b1, b3, tag="part1_0")
         turn_back(0, b0)
         store(nc.scalar, 0, b0)
         gated_pair = held.tile([P, 2 * (b1 - b0)], F32, name="gated_pair")
         nc.vector.tensor_tensor(gated_pair[:].rearrange("p (r t) -> p r t", r=2), pair[:], gates[:, 1:3, b0:b1], MULT)
         part[1, b0] = (gated_pair, 0)
         part[2, b0] = (gated_pair, b1 - b0)
-        apply_gate(0, b1, b3)
-        add_two(0, 1, b0, b1)
         apply_gate(1, b1, b3)
+        add_two(0, 1, b0, b1)
+        add_two(0, 1, b1, b3)
+        apply_gate(2, b1, b3)
         add_third(2, b0, b1)
         store(nc.sync, b0, b1)
-        add_two(0, 1, b1, b3)
-        apply_gate(2, b1, b2)
-        apply_gate(2, b2, b3)
-        add_third(2, b1, b2)
-        add_third(2, b2, b3)
+        add_third(2, b1, b3)
         store(nc.sync, b1, b3)

@@ -45,7 +45,7 @@ def tile_moe_tk_lin_silu_kernel(
     nc = tc.nc
     with ExitStack() as ctx:
         held = ctx.enter_context(tc.tile_pool(name="held", bufs=1))
-        psum = ctx.enter_context(tc.psum_pool(name="psum", bufs=8))
+        psum = ctx.enter_context(tc.psum_pool(name="psum", bufs=4))
 
         offs_t = held.tile([P, S // 16], U16, name="offs_t")
         pos_t = [held.tile([P, T // 16], U16, name=f"pos_t{r}") for r in range(TOP)]
@@ -140,7 +140,7 @@ def tile_moe_tk_lin_silu_kernel(
             late = held.tile([P, s1 - s0], U32, name=f"held_back{a}_{s0}", tag=tag, align_bytes=64)
             nc.vector.tensor_copy(out=late[:], in_=words_of(a, s0, s1))
             for s in range(s0, s1, GROUP):
-                held_back[a, s] = late[:, s - s0 : s - s0 + GROUP]
+                held_back[a, s] = (late, s - s0)
 
         def gather_scale_bytes(s0, s1):
             nc.vector.tensor_copy(out=slot_planes[:, s0:s1], in_=planes[:].indirect(offs_t[:, s0 // 16 : s1 // 16]))
@@ -170,32 +170,47 @@ def tile_moe_tk_lin_silu_kernel(
         gather_scale_bytes(3 * QUARTER, S)
         gather_words(2, 2 * QUARTER, 3 * QUARTER)
         gather_held_back_words(1, 3 * QUARTER, S, "rounded2_512")
-        gather_words(2, 3 * QUARTER, S - 2 * GROUP)
+        gather_words(2, 3 * QUARTER, S - 2 * C)
+        gather_words(2, S - 2 * C, S - C)
         gather_words(2, S - 2 * GROUP, S - GROUP)
         gather_words(2, S - GROUP, S)
 
         y = held.tile([P, S], F32, name="y")
-        for s0 in range(0, S, GROUP):
+        def one_pass(acc, a, s0, width):
             e = s0 // C
-            cols = slice(s0, s0 + GROUP)
-            acc = psum.tile([P, GROUP], F32, name="bank")
-            for a in range(PASSES):
-                if a == 0:
-                    weights, weight_plane = w8[:, e, :].bitcast(FP8X4), w8_plane[:, e, :]
-                else:
-                    m = 2 * e + a - 1
-                    weights, weight_plane = w4[:, m, :].bitcast(FP4X4), w4_plane[:, m, :]
-                words = slot_codes[a][:, cols] if s0 < EARLY[a] else held_back[a, s0]
-                nc.tensor.matmul_mx(
-                    out=acc[:],
-                    lhsT=weights,
-                    lhsT_scale=weight_plane,
-                    rhs=words.bitcast(FP8X4),
-                    rhs_scale=moved_plane[:, cols] if a == 2 else slot_planes[FIRST_ROW[a] : P, cols],
-                    start=(a == 0),
-                    stop=(a == PASSES - 1),
+            cols = slice(s0, s0 + width)
+            if a == 0:
+                weights, weight_plane = w8[:, e, :].bitcast(FP8X4), w8_plane[:, e, :]
+            else:
+                m = 2 * e + a - 1
+                weights, weight_plane = w4[:, m, :].bitcast(FP4X4), w4_plane[:, m, :]
+            if s0 < EARLY[a]:
+                words = slot_codes[a][:, cols]
+            else:
+                late, u = held_back[a, s0]
+                words = late[:, u : u + width]
+            nc.tensor.matmul_mx(
+                out=acc[:],
+                lhsT=weights,
+                lhsT_scale=weight_plane,
+                rhs=words.bitcast(FP8X4),
+                rhs_scale=moved_plane[:, cols] if a == 2 else slot_planes[FIRST_ROW[a] : P, cols],
+                start=(a == 0),
+                stop=(a == PASSES - 1),
+            )
+
+        groups = [(s, C) for s in range(0, S - C, C)] + [(s, GROUP) for s in range(S - C, S, GROUP)]
+        for q in range(0, S, QUARTER):
+            mine = [(s0, width) for s0, width in groups if q <= s0 < q + QUARTER]
+            acc = {s0: psum.tile([P, width], F32, name="bank") for s0, width in mine}
+            for a in range(PASSES - 1):
+                for s0, width in mine:
+                    one_pass(acc[s0], a, s0, width)
+            for s0, width in mine:
+                one_pass(acc[s0], PASSES - 1, s0, width)
+                nc.scalar.activation(
+                    out=y[:, s0 : s0 + width], in_=acc[s0][:], func=SILU, bias=bias[:, s0 // C : s0 // C + 1]
                 )
-            nc.scalar.activation(out=y[:, cols], in_=acc[:], func=SILU, bias=bias[:, e : e + 1])
 
         part = {}
         plain = {}

@@ -136,10 +136,10 @@ def tile_moe_tk_lin_silu_kernel(
         def gather_words(a, s0, s1):
             nc.vector.tensor_copy(out=slot_codes[a][:, s0:s1], in_=words_of(a, s0, s1))
 
-        def gather_held_back_words(a, s0, s1, tag):
-            late = held.tile([P, s1 - s0], U32, name=f"held_back{a}_{s0}", tag=tag, align_bytes=64)
-            nc.vector.tensor_copy(out=late[:], in_=words_of(a, s0, s1))
-            for s in range(s0, s1, GROUP):
+        def gather_held_back_words(a, s0, s1, tag, room=None):
+            late = held.tile([P, room or s1 - s0], U32, name=f"held_back{a}_{s0}", tag=tag, align_bytes=64)
+            nc.vector.tensor_copy(out=late[:, 0 : s1 - s0], in_=words_of(a, s0, s1))
+            for s in range(s0, s0 + (room or s1 - s0), GROUP):
                 held_back[a, s] = (late, s - s0)
 
         def gather_scale_bytes(s0, s1):
@@ -169,9 +169,10 @@ def tile_moe_tk_lin_silu_kernel(
         gather_words(2, QUARTER, 2 * QUARTER)
         gather_scale_bytes(3 * QUARTER, S)
         gather_words(2, 2 * QUARTER, 3 * QUARTER)
-        gather_held_back_words(1, 3 * QUARTER, S, "rounded2_512")
-        gather_words(2, 3 * QUARTER, S - 2 * C)
-        gather_words(2, S - 2 * C, S - C)
+        gather_held_back_words(1, 3 * QUARTER, S - C, "rounded2_512", room=QUARTER)
+        gather_words(2, 3 * QUARTER, S - C)
+        late, u = held_back[1, S - C]
+        nc.vector.tensor_copy(out=late[:, u : u + C], in_=words_of(1, S - C, S))
         gather_words(2, S - 2 * GROUP, S - GROUP)
         gather_words(2, S - GROUP, S)
 
@@ -200,8 +201,8 @@ def tile_moe_tk_lin_silu_kernel(
             )
 
         groups = [(s, C) for s in range(0, S - C, C)] + [(s, GROUP) for s in range(S - C, S, GROUP)]
-        for q in range(0, S, QUARTER):
-            mine = [(s0, width) for s0, width in groups if q <= s0 < q + QUARTER]
+        for q0, q1 in ((0, QUARTER), (QUARTER, 2 * QUARTER), (2 * QUARTER, 3 * QUARTER), (3 * QUARTER, S - C), (S - C, S)):
+            mine = [(s0, width) for s0, width in groups if q0 <= s0 < q1]
             acc = {s0: psum.tile([P, width], F32, name="bank") for s0, width in mine}
             for a in range(PASSES - 1):
                 for s0, width in mine:

@@ -51,7 +51,7 @@ def tile_moe_tk_lin_silu_kernel(
         pos_t = [held.tile([P, T // 16], U16, name=f"pos_t{r}") for r in range(TOP)]
 
         planes = held.tile([P, 2 * T], U8, name="planes", align_bytes=64)
-        codes = [held.tile([P, (2 * T, 4 * T, T)[a]], U32, name=f"codes{a}", align_bytes=64) for a in range(PASSES)]
+        codes = [held.tile([P, (2 * T, 4 * T, 2 * T)[a]], U32, name=f"codes{a}", align_bytes=64) for a in range(PASSES)]
         moved_plane = held.tile([P, S], U8, name="moved_plane", align_bytes=64)
         w8_plane = held.tile([P, E, N], U8, name="w8_plane", align_bytes=64)
         w4_plane = held.tile([P, 2 * E, N], U8, name="w4_plane", align_bytes=64)
@@ -90,9 +90,16 @@ def tile_moe_tk_lin_silu_kernel(
                 in_=w4_scales[:, :, 4 * q : 4 * q + 4, :].rearrange("e a q n -> q (e a) n").bitcast(I32),
             )
         w8 = held.tile([P, E, 4 * N], U8, name="w8", align_bytes=64)
-        nc.sync.dma_start(out=w8[:].bitcast(I32), in_=w8_words.rearrange("e a p n r -> p (e a) (n r)").bitcast(I32))
         w4 = held.tile([P, 2 * E, 2 * N], U8, name="w4", align_bytes=64)
-        nc.sync.dma_start(out=w4[:].bitcast(I32), in_=w4_words.rearrange("e a p m -> p (e a) m").bitcast(I32))
+        for e0 in (0, E // 2):
+            nc.sync.dma_start(
+                out=w8[:, e0 : e0 + E // 2, :].bitcast(I32),
+                in_=w8_words[e0 : e0 + E // 2].rearrange("e a p n r -> p (e a) (n r)").bitcast(I32),
+            )
+            nc.sync.dma_start(
+                out=w4[:, 2 * e0 : 2 * e0 + E, :].bitcast(I32),
+                in_=w4_words[e0 : e0 + E // 2].rearrange("e a p m -> p (e a) m").bitcast(I32),
+            )
         bias = held.tile([P, E], F32, name="bias")
         nc.sync.dma_start(out=bias[:], in_=b)
         for r, pos in enumerate((pos1, pos2, pos3)):
@@ -161,13 +168,12 @@ def tile_moe_tk_lin_silu_kernel(
         gather_held_back_words(1, EARLY[1], EARLY[1] + SPACER, "raw2_512")
 
         gates = held.tile([P, TOP, T], F32, name="gates", tag="rounded2_0", align_bytes=64)
-        nc.scalar.dma_start(out=gates[:], in_=gate.rearrange("r p t -> p r t"))
+        for r in range(TOP):
+            nc.scalar.dma_start(out=gates[:, r, :], in_=gate[r])
 
-        gather_scale_bytes(0, QUARTER)
-        gather_words(2, 0, QUARTER)
-        gather_scale_bytes(QUARTER, 3 * QUARTER)
-        gather_words(2, QUARTER, 2 * QUARTER)
-        gather_scale_bytes(3 * QUARTER, S)
+        gather_scale_bytes(0, S // 2)
+        gather_words(2, 0, S // 2)
+        gather_scale_bytes(S // 2, S)
         gather_words(2, 2 * QUARTER, 3 * QUARTER)
         gather_held_back_words(1, 3 * QUARTER, S - C, "rounded2_512", room=QUARTER)
         gather_words(2, 3 * QUARTER, S - C)

@@ -35,7 +35,7 @@ GROUP = 128
 SPACER = 256
 EARLY = (S - SPACER, 2048, S)
 QUARTER = S // 4
-ON_TENSOR = 512
+TURNED = 512
 HALF = 256
 
 
@@ -46,6 +46,7 @@ def tile_moe_tk_lin_silu_kernel(
     with ExitStack() as ctx:
         held = ctx.enter_context(tc.tile_pool(name="held", bufs=1))
         psum = ctx.enter_context(tc.psum_pool(name="psum", bufs=4))
+        psum_end = ctx.enter_context(tc.psum_pool(name="psum_end", bufs=1))
 
         offs_t = held.tile([P, S // 16], U16, name="offs_t")
         pos_t = [held.tile([P, T // 16], U16, name=f"pos_t{r}") for r in range(TOP)]
@@ -91,19 +92,19 @@ def tile_moe_tk_lin_silu_kernel(
             )
         w8 = held.tile([P, E, 4 * N], U8, name="w8", align_bytes=64)
         w4 = held.tile([P, 2 * E, 2 * N], U8, name="w4", align_bytes=64)
-        for e0 in (0, E // 2):
-            nc.sync.dma_start(
-                out=w8[:, e0 : e0 + E // 2, :].bitcast(I32),
-                in_=w8_words[e0 : e0 + E // 2].rearrange("e a p n r -> p (e a) (n r)").bitcast(I32),
-            )
-            nc.sync.dma_start(
-                out=w4[:, 2 * e0 : 2 * e0 + E, :].bitcast(I32),
-                in_=w4_words[e0 : e0 + E // 2].rearrange("e a p m -> p (e a) m").bitcast(I32),
-            )
+        nc.sync.dma_start(
+            out=w8[:].bitcast(I32), in_=w8_words.rearrange("e a p n r -> p (e a) (n r)").bitcast(I32)
+        )
+        nc.sync.dma_start(out=w4[:].bitcast(I32), in_=w4_words.rearrange("e a p m -> p (e a) m").bitcast(I32))
         bias = held.tile([P, E], F32, name="bias")
         nc.sync.dma_start(out=bias[:], in_=b)
         for r, pos in enumerate((pos1, pos2, pos3)):
             nc.sync.dma_start(pos_t[r][:], pos)
+        gate_columns = {}
+        for r in (1, 2):
+            gate_columns[r] = held.tile([P, TURNED // P], F32, name=f"gate_columns{r}")
+            with nc.allow_non_contiguous_dma(reason="one gate a partition"):
+                nc.sync.dma_start(out=gate_columns[r][:], in_=gate[r, 0, 0:TURNED].rearrange("(c p) -> p c", p=P))
 
         slot_codes = [held.tile([P, EARLY[a]], U32, name=f"slot_codes{a}", align_bytes=64) for a in range(PASSES)]
         slot_planes = held.tile([P, S], U8, name="slot_planes", align_bytes=64)
@@ -167,9 +168,11 @@ def tile_moe_tk_lin_silu_kernel(
         round_and_quantise(2)
         gather_held_back_words(1, EARLY[1], EARLY[1] + SPACER, "raw2_512")
 
-        gates = held.tile([P, TOP, T], F32, name="gates", tag="rounded2_0", align_bytes=64)
-        for r in range(TOP):
-            nc.scalar.dma_start(out=gates[:, r, :], in_=gate[r])
+        gates = held.tile([P, T + 2 * (T - TURNED)], F32, name="gates", tag="rounded2_0", align_bytes=64)
+        nc.scalar.dma_start(out=gates[:, 0:T], in_=gate[0])
+        nc.scalar.dma_start(
+            out=gates[:, T:].rearrange("p (r t) -> p r t", r=2), in_=gate[1:TOP, :, TURNED:T].rearrange("r p t -> p r t")
+        )
 
         gather_scale_bytes(0, S // 2)
         gather_words(2, 0, S // 2)
@@ -219,98 +222,74 @@ def tile_moe_tk_lin_silu_kernel(
                     out=y[:, s0 : s0 + width], in_=acc[s0][:], func=SILU, bias=bias[:, s0 // C : s0 // C + 1]
                 )
 
-        part = {}
-        plain = {}
-
         def results_of(r, t0, t1):
             return y[:].indirect(pos_t[r][:, t0 // 16 : t1 // 16])
 
-        def new_part(r, t0, t1):
-            tile = held.tile([P, t1 - t0], F32, name=f"part{r}_{t0}", tag=f"part{r}_{t0}")
-            for t in range(t0, t1, 64):
-                part[r, t] = (tile, t - t0)
-            return tile
-
-        def part_of(r, t0, t1):
-            tile, u = part[r, t0]
-            return tile[:, u : u + t1 - t0]
+        def gates_of(r, t0, t1):
+            first = T + (r - 1) * (T - TURNED) - TURNED if r else 0
+            return gates[:, first + t0 : first + t1]
 
         def fetch_gated(r, t0, t1):
-            nc.vector.tensor_tensor(new_part(r, t0, t1)[:], results_of(r, t0, t1), gates[:, r, t0:t1], MULT)
+            part = held.tile([P, t1 - t0], F32, name=f"part{r}_{t0}")
+            nc.vector.tensor_tensor(part[:], results_of(r, t0, t1), gates_of(r, t0, t1), MULT)
+            return part
 
         def fetch_plain(r, t0, t1, tag=None):
-            tile = held.tile([P, t1 - t0], F32, name=f"plain{r}_{t0}", tag=tag or f"plain{r}_{t0}")
-            for t in range(t0, t1, 64):
-                plain[r, t] = (tile, t - t0)
-            nc.scalar.activation(out=tile[:], in_=results_of(r, t0, t1), func=COPY)
+            plain = held.tile([P, t1 - t0], F32, name=f"plain{r}_{t0}", tag=tag or f"plain{r}_{t0}")
+            nc.scalar.activation(out=plain[:], in_=results_of(r, t0, t1), func=COPY)
+            return plain
 
-        def apply_gate(r, t0, t1):
-            tile, u = plain[r, t0]
-            nc.vector.tensor_tensor(new_part(r, t0, t1)[:], tile[:, u : u + t1 - t0], gates[:, r, t0:t1], MULT)
+        def fetch_and_turn(t0):
+            turned = psum_end.tile([P, 2, HALF], F32, name=f"turned{t0}")
+            for r in (1, 2):
+                plain = fetch_plain(r, t0, t0 + HALF)
+                for u in range(0, HALF, P):
+                    nc.tensor.transpose(turned[:, r - 1, u : u + P], plain[:, u : u + P], identity[:])
+            return turned
 
-        turned = {}
-        sums = {}
-        result = held.tile([P, T], F32, name="result")
-        first_two = held.tile([P, T], F32, name="first_two")
-
-        def turn(r, t0, t1, first=False, last=False):
-            if first:
-                turned[0] = psum.tile([P, t1 - t0], F32, name="bank")
-            for t in range(t0, t1, P):
+        def gate_and_turn_back(t0, turned):
+            back = psum_end.tile([P, HALF], F32, name=f"back{t0}")
+            steps = [(r, u) for r in (1, 2) for u in range(0, HALF, P)]
+            for r, u in steps:
+                c = (t0 + u) // P
+                gated = held.tile([P, P], F32, name=f"gated{r}_{c}")
+                nc.scalar.activation(
+                    out=gated[:], in_=turned[:, r - 1, u : u + P], func=COPY, scale=gate_columns[r][:, c : c + 1]
+                )
                 nc.tensor.matmul(
-                    turned[0][:, t : t + P],
-                    lhsT=part_of(r, t, t + P),
+                    back[:, u : u + P],
+                    lhsT=gated[:],
                     rhs=identity[:],
                     is_transpose=True,
-                    start=(first and t == t0),
-                    stop=(last and t == t1 - P),
+                    start=((r, u) == steps[0]),
+                    stop=((r, u) == steps[-1]),
                 )
+            return back
 
-        def copy_sums(t0, t1):
-            sums[t0] = held.tile([P, t1 - t0], F32, name=f"sums{t0}")
-            nc.scalar.copy(out=sums[t0][:], in_=turned[t0][:])
-
-        def turn_back(t0, t1):
-            back = psum.tile([P, t1 - t0], F32, name="bank")
-            for u in range(0, t1 - t0, P):
-                nc.tensor.transpose(back[:, u : u + P], sums[t0][:, u : u + P], identity[:])
-            nc.scalar.copy(out=result[:, t0:t1], in_=back[:])
-
-        def add_two(r0, r1, t0, t1):
-            nc.vector.tensor_add(first_two[:, t0:t1], part_of(r0, t0, t1), part_of(r1, t0, t1))
-
-        def add_third(r, t0, t1):
-            nc.vector.tensor_add(result[:, t0:t1], first_two[:, t0:t1], part_of(r, t0, t1))
+        result = held.tile([P, T], F32, name="result")
 
         def store(queue, t0, t1):
             queue.dma_start(out=out[:, t0:t1], in_=result[:, t0:t1])
 
-        b0, b1, b3 = 384, 768, T
-        fetch_plain(1, 0, b0)
-        fetch_gated(0, 0, b0)
-        fetch_gated(2, 0, b0)
-        apply_gate(1, 0, b0)
-        fetch_gated(0, b0, b3)
-        turn(0, 0, b0, first=True)
-        turn(2, 0, b0)
-        turn(1, 0, b0, last=True)
-        pair = held.tile([P, 2, b1 - b0], F32, name="pair")
-        for r in (1, 2):
-            nc.scalar.activation(out=pair[:, r - 1, :], in_=results_of(r, b0, b1), func=COPY)
-        fetch_plain(1, b1, b3)
-        copy_sums(0, b0)
-        fetch_plain(2, b1, b3, tag="part1_0")
-        turn_back(0, b0)
-        store(nc.scalar, 0, b0)
-        gated_pair = held.tile([P, 2 * (b1 - b0)], F32, name="gated_pair")
-        nc.vector.tensor_tensor(gated_pair[:].rearrange("p (r t) -> p r t", r=2), pair[:], gates[:, 1:3, b0:b1], MULT)
-        part[1, b0] = (gated_pair, 0)
-        part[2, b0] = (gated_pair, b1 - b0)
-        apply_gate(1, b1, b3)
-        add_two(0, 1, b0, b1)
-        add_two(0, 1, b1, b3)
-        apply_gate(2, b1, b3)
-        add_third(2, b0, b1)
-        store(nc.sync, b0, b1)
-        add_third(2, b1, b3)
-        store(nc.sync, b1, b3)
+        ta, tb, tc_, td = 0, HALF, TURNED, TURNED + HALF
+        turned_a = fetch_and_turn(ta)
+        turned_b = fetch_and_turn(tb)
+        first_ab = fetch_gated(0, 0, TURNED)
+        first_cd = fetch_gated(0, TURNED, T)
+        third_cd = fetch_gated(2, TURNED, T)
+        second_d = fetch_gated(1, td, T)
+        back_a = gate_and_turn_back(ta, turned_a)
+        back_b = gate_and_turn_back(tb, turned_b)
+        plain_c = fetch_plain(1, tc_, td, tag=f"plain2_{tb}")
+        two_cd = held.tile([P, T - TURNED], F32, name="two_cd")
+        nc.vector.tensor_add(two_cd[:], first_cd[:], third_cd[:])
+        nc.vector.tensor_add(result[:, ta:tb], back_a[:], first_ab[:, ta:tb])
+        store(nc.sync, ta, tb)
+        nc.vector.tensor_add(result[:, td:T], two_cd[:, HALF:], second_d[:])
+        store(nc.sync, td, T)
+        second_c = held.tile([P, HALF], F32, name="second_c")
+        nc.vector.tensor_tensor(second_c[:], plain_c[:], gates_of(1, tc_, td), MULT)
+        nc.vector.tensor_add(result[:, tb:tc_], back_b[:], first_ab[:, tb:tc_])
+        store(nc.scalar, tb, tc_)
+        nc.vector.tensor_add(result[:, tc_:td], two_cd[:, 0:HALF], second_c[:])
+        store(nc.sync, tc_, td)

@@ -36,6 +36,7 @@ SPACER = 256
 EARLY = (S - SPACER, 2048, S)
 QUARTER = S // 4
 TURNED = 512
+BLOCKS = TURNED // P
 HALF = 256
 
 
@@ -68,6 +69,8 @@ def tile_moe_tk_lin_silu_kernel(
 
         identity = held.tile([P, P], F32, name="identity")
         make_identity(nc, identity[:])
+        gate_rows = held.tile([P, P], F32, name="gate_rows")
+        nc.gpsimd.memset(gate_rows[:], 0.0)
 
         raw = {}
         for a in range(PASSES):
@@ -81,6 +84,14 @@ def tile_moe_tk_lin_silu_kernel(
                 t0 = t0 + n
             if a == 0:
                 nc.sync.dma_start(offs_t[:], offs)
+        for r in (1, 2):
+            nc.sync.dma_start(
+                out=gate_rows[BLOCKS * (r - 1) : BLOCKS * r, :], in_=gate[r, 0, 0:TURNED].rearrange("(c p) -> c p", p=P)
+            )
+        gates_turned = psum_end.tile([P, P], F32, name="gates_turned", tag="back0")
+        nc.tensor.transpose(gates_turned[:], gate_rows[:], identity[:])
+        gate_columns = held.tile([P, 2 * BLOCKS], F32, name="gate_columns")
+        nc.scalar.copy(out=gate_columns[:], in_=gates_turned[:, 0 : 2 * BLOCKS])
         for q in range(4):
             nc.sync.dma_start(
                 out=w8_plane[32 * q : 32 * q + 4, :, :].bitcast(I32),
@@ -100,11 +111,6 @@ def tile_moe_tk_lin_silu_kernel(
         nc.sync.dma_start(out=bias[:], in_=b)
         for r, pos in enumerate((pos1, pos2, pos3)):
             nc.sync.dma_start(pos_t[r][:], pos)
-        gate_columns = {}
-        for r in (1, 2):
-            gate_columns[r] = held.tile([P, TURNED // P], F32, name=f"gate_columns{r}")
-            with nc.allow_non_contiguous_dma(reason="one gate a partition"):
-                nc.sync.dma_start(out=gate_columns[r][:], in_=gate[r, 0, 0:TURNED].rearrange("(c p) -> p c", p=P))
 
         slot_codes = [held.tile([P, EARLY[a]], U32, name=f"slot_codes{a}", align_bytes=64) for a in range(PASSES)]
         slot_planes = held.tile([P, S], U8, name="slot_planes", align_bytes=64)
@@ -248,13 +254,14 @@ def tile_moe_tk_lin_silu_kernel(
             return turned
 
         def gate_and_turn_back(t0, turned):
-            back = psum_end.tile([P, HALF], F32, name=f"back{t0}")
+            back = psum_end.tile([P, HALF], F32, name=f"back{t0}", tag=f"back{t0}")
             steps = [(r, u) for r in (1, 2) for u in range(0, HALF, P)]
             for r, u in steps:
                 c = (t0 + u) // P
+                m = BLOCKS * (r - 1) + c
                 gated = held.tile([P, P], F32, name=f"gated{r}_{c}")
                 nc.scalar.activation(
-                    out=gated[:], in_=turned[:, r - 1, u : u + P], func=COPY, scale=gate_columns[r][:, c : c + 1]
+                    out=gated[:], in_=turned[:, r - 1, u : u + P], func=COPY, scale=gate_columns[:, m : m + 1]
                 )
                 nc.tensor.matmul(
                     back[:, u : u + P],

@@ -286,17 +286,17 @@ def tile_moe_tk_lin_silu_kernel(
         third_cd = fetch_gated(2, TURNED, T)
         second_d = fetch_gated(1, td, T)
         back_a = gate_and_turn_back(ta, turned_a)
+        plain_c = fetch_plain(1, tc_, td, tag=f"plain2_{ta}")
         back_b = gate_and_turn_back(tb, turned_b)
-        plain_c = fetch_plain(1, tc_, td, tag=f"plain2_{tb}")
         two_cd = held.tile([P, T - TURNED], F32, name="two_cd")
         nc.vector.tensor_add(two_cd[:], first_cd[:], third_cd[:])
-        nc.vector.tensor_add(result[:, ta:tb], back_a[:], first_ab[:, ta:tb])
-        store(nc.sync, ta, tb)
-        nc.vector.tensor_add(result[:, td:T], two_cd[:, HALF:], second_d[:])
-        store(nc.sync, td, T)
         second_c = held.tile([P, HALF], F32, name="second_c")
         nc.vector.tensor_tensor(second_c[:], plain_c[:], gates_of(1, tc_, td), MULT)
-        nc.vector.tensor_add(result[:, tb:tc_], back_b[:], first_ab[:, tb:tc_])
-        store(nc.scalar, tb, tc_)
+        nc.vector.tensor_add(result[:, td:T], two_cd[:, HALF:], second_d[:])
+        store(nc.sync, td, T)
+        nc.vector.tensor_add(result[:, ta:tb], back_a[:], first_ab[:, ta:tb])
+        store(nc.sync, ta, tb)
         nc.vector.tensor_add(result[:, tc_:td], two_cd[:, 0:HALF], second_c[:])
         store(nc.sync, tc_, td)
+        nc.vector.tensor_add(result[:, tb:tc_], back_b[:], first_ab[:, tb:tc_])
+        store(nc.sync, tb, tc_)

@@ -281,22 +281,21 @@ def tile_moe_tk_lin_silu_kernel(
         ta, tb, tc_, td = 0, HALF, TURNED, TURNED + HALF
         turned_a = fetch_and_turn(ta)
         turned_b = fetch_and_turn(tb)
-        first_ab = fetch_gated(0, 0, TURNED)
-        first_cd = fetch_gated(0, TURNED, T)
+        first = fetch_gated(0, 0, T)
         third_cd = fetch_gated(2, TURNED, T)
         second_d = fetch_gated(1, td, T)
         back_a = gate_and_turn_back(ta, turned_a)
         plain_c = fetch_plain(1, tc_, td, tag=f"plain2_{ta}")
         back_b = gate_and_turn_back(tb, turned_b)
         two_cd = held.tile([P, T - TURNED], F32, name="two_cd")
-        nc.vector.tensor_add(two_cd[:], first_cd[:], third_cd[:])
+        nc.vector.tensor_add(two_cd[:], first[:, TURNED:T], third_cd[:])
         second_c = held.tile([P, HALF], F32, name="second_c")
         nc.vector.tensor_tensor(second_c[:], plain_c[:], gates_of(1, tc_, td), MULT)
         nc.vector.tensor_add(result[:, td:T], two_cd[:, HALF:], second_d[:])
         store(nc.sync, td, T)
-        nc.vector.tensor_add(result[:, ta:tb], back_a[:], first_ab[:, ta:tb])
+        nc.vector.tensor_add(result[:, ta:tb], back_a[:], first[:, ta:tb])
         store(nc.sync, ta, tb)
         nc.vector.tensor_add(result[:, tc_:td], two_cd[:, 0:HALF], second_c[:])
         store(nc.sync, tc_, td)
-        nc.vector.tensor_add(result[:, tb:tc_], back_b[:], first_ab[:, tb:tc_])
+        nc.vector.tensor_add(result[:, tb:tc_], back_b[:], first[:, tb:tc_])
         store(nc.sync, tb, tc_)

@@ -52,17 +52,19 @@ def tile_moe_tk_lin_silu_kernel(
         offs_t = held.tile([P, S // 16], U16, name="offs_t")
         pos_t = [held.tile([P, T // 16], U16, name=f"pos_t{r}") for r in range(TOP)]
 
-        planes = held.tile([P, 2 * T], U8, name="planes", align_bytes=64)
+        planes = held.tile([P, 4 * T], U8, name="planes", align_bytes=64)
         codes = [held.tile([P, (2 * T, 4 * T, 2 * T)[a]], U32, name=f"codes{a}", align_bytes=64) for a in range(PASSES)]
         moved_plane = held.tile([P, S], U8, name="moved_plane", align_bytes=64)
         w8_plane = held.tile([P, E, N], U8, name="w8_plane", align_bytes=64)
         w4_plane = held.tile([P, 2 * E, N], U8, name="w4_plane", align_bytes=64)
         warm_in = held.tile([P, 1], F32, name="warm_in")
         nc.vector.memset(warm_in[:], 0.0)
-        nc.vector.memset(planes[:, 0:T].bitcast(I32), 0)
+        for t0 in (0, T // 2):
+            nc.vector.memset(planes[:, t0 : t0 + T // 2].bitcast(I32), 0)
         nc.vector.memset(w8_plane[:].rearrange("p e n -> p (e n)").bitcast(I32), 0)
         nc.vector.memset(w4_plane[:].rearrange("p e n -> p (e n)").bitcast(I32), 0)
-        nc.vector.memset(moved_plane[:].bitcast(I32), 0)
+        for s0, s1 in ((0, EARLY[1]), (EARLY[1], S)):
+            nc.vector.memset(moved_plane[:, s0:s1].bitcast(I32), 0)
 
         warm_out = held.tile([P, 1], F32, name="warm_out")
         nc.scalar.activation(out=warm_out[:], in_=warm_in[:], func=SILU)
@@ -172,7 +174,7 @@ def tile_moe_tk_lin_silu_kernel(
         gather_held_back_words(0, EARLY[0], S, "raw1_768")
         gather_words(1, 0, EARLY[1])
         round_and_quantise(2)
-        gather_held_back_words(1, EARLY[1], EARLY[1] + SPACER, "raw2_512")
+        gather_held_back_words(1, EARLY[1], S - C, "raw2_512")
 
         gates = held.tile([P, T + 2 * (T - TURNED)], F32, name="gates", tag="rounded2_0", align_bytes=64)
         nc.scalar.dma_start(out=gates[:, 0:T], in_=gate[0])
@@ -180,14 +182,12 @@ def tile_moe_tk_lin_silu_kernel(
             out=gates[:, T:].rearrange("p (r t) -> p r t", r=2), in_=gate[1:TOP, :, TURNED:T].rearrange("r p t -> p r t")
         )
 
-        gather_scale_bytes(0, S // 2)
+        gather_scale_bytes(0, EARLY[1])
         gather_words(2, 0, S // 2)
-        gather_scale_bytes(S // 2, S)
+        gather_scale_bytes(EARLY[1], S)
         gather_words(2, 2 * QUARTER, 3 * QUARTER)
-        gather_held_back_words(1, 3 * QUARTER, S - C, "rounded2_512", room=QUARTER)
         gather_words(2, 3 * QUARTER, S - C)
-        late, u = held_back[1, S - C]
-        nc.vector.tensor_copy(out=late[:, u : u + C], in_=words_of(1, S - C, S))
+        gather_held_back_words(1, S - C, S, "rounded2_512")
         gather_words(2, S - 2 * GROUP, S - GROUP)
         gather_words(2, S - GROUP, S)
 

@@ -59,12 +59,10 @@ def tile_moe_tk_lin_silu_kernel(
         w4_plane = held.tile([P, 2 * E, N], U8, name="w4_plane", align_bytes=64)
         warm_in = held.tile([P, 1], F32, name="warm_in")
         nc.vector.memset(warm_in[:], 0.0)
-        for t0 in (0, T // 2):
-            nc.vector.memset(planes[:, t0 : t0 + T // 2].bitcast(I32), 0)
+        nc.vector.memset(planes[:, 0:T].bitcast(I32), 0)
         nc.vector.memset(w8_plane[:].rearrange("p e n -> p (e n)").bitcast(I32), 0)
         nc.vector.memset(w4_plane[:].rearrange("p e n -> p (e n)").bitcast(I32), 0)
-        for s0, s1 in ((0, EARLY[1]), (EARLY[1], S)):
-            nc.vector.memset(moved_plane[:, s0:s1].bitcast(I32), 0)
+        nc.vector.memset(moved_plane[:].bitcast(I32), 0)
 
         warm_out = held.tile([P, 1], F32, name="warm_out")
         nc.scalar.activation(out=warm_out[:], in_=warm_in[:], func=SILU)
@@ -281,21 +279,22 @@ def tile_moe_tk_lin_silu_kernel(
         ta, tb, tc_, td = 0, HALF, TURNED, TURNED + HALF
         turned_a = fetch_and_turn(ta)
         turned_b = fetch_and_turn(tb)
-        first = fetch_gated(0, 0, T)
-        third_cd = fetch_gated(2, TURNED, T)
         second_d = fetch_gated(1, td, T)
+        third_cd = fetch_gated(2, TURNED, T)
+        first = fetch_gated(0, 0, T)
         back_a = gate_and_turn_back(ta, turned_a)
         plain_c = fetch_plain(1, tc_, td, tag=f"plain2_{ta}")
         back_b = gate_and_turn_back(tb, turned_b)
         two_cd = held.tile([P, T - TURNED], F32, name="two_cd")
-        nc.vector.tensor_add(two_cd[:], first[:, TURNED:T], third_cd[:])
-        second_c = held.tile([P, HALF], F32, name="second_c")
-        nc.vector.tensor_tensor(second_c[:], plain_c[:], gates_of(1, tc_, td), MULT)
-        nc.vector.tensor_add(result[:, td:T], two_cd[:, HALF:], second_d[:])
+        nc.vector.tensor_add(two_cd[:, HALF:], third_cd[:, HALF:], second_d[:])
+        nc.vector.tensor_add(two_cd[:, 0:HALF], third_cd[:, 0:HALF], first[:, tc_:td])
+        nc.vector.tensor_add(result[:, td:T], two_cd[:, HALF:], first[:, td:T])
         store(nc.sync, td, T)
         nc.vector.tensor_add(result[:, ta:tb], back_a[:], first[:, ta:tb])
         store(nc.sync, ta, tb)
-        nc.vector.tensor_add(result[:, tc_:td], two_cd[:, 0:HALF], second_c[:])
-        store(nc.sync, tc_, td)
+        second_c = held.tile([P, HALF], F32, name="second_c")
+        nc.vector.tensor_tensor(second_c[:], plain_c[:], gates_of(1, tc_, td), MULT)
         nc.vector.tensor_add(result[:, tb:tc_], back_b[:], first[:, tb:tc_])
         store(nc.sync, tb, tc_)
+        nc.vector.tensor_add(result[:, tc_:td], two_cd[:, 0:HALF], second_c[:])
+        store(nc.sync, tc_, td)

@@ -60,8 +60,10 @@ def tile_moe_tk_lin_silu_kernel(
         warm_in = held.tile([P, 1], F32, name="warm_in")
         nc.vector.memset(warm_in[:], 0.0)
         nc.vector.memset(planes[:, 0:T].bitcast(I32), 0)
-        nc.vector.memset(w8_plane[:].rearrange("p e n -> p (e n)").bitcast(I32), 0)
-        nc.vector.memset(w4_plane[:].rearrange("p e n -> p (e n)").bitcast(I32), 0)
+        for e in range(E):
+            nc.vector.memset(w8_plane[:, e, :].bitcast(I32), 0)
+        for e in range(0, E, 4):
+            nc.vector.memset(w4_plane[:, 2 * e : 2 * e + 8, :].rearrange("p e n -> p (e n)").bitcast(I32), 0)
         nc.vector.memset(moved_plane[:].bitcast(I32), 0)
 
         warm_out = held.tile([P, 1], F32, name="warm_out")
@@ -175,8 +177,8 @@ def tile_moe_tk_lin_silu_kernel(
         gather_held_back_words(1, EARLY[1], S - C, "raw2_512")
 
         gates = held.tile([P, T + 2 * (T - TURNED)], F32, name="gates", tag="rounded2_0", align_bytes=64)
-        nc.scalar.dma_start(out=gates[:, 0:T], in_=gate[0])
-        nc.scalar.dma_start(
+        nc.sync.dma_start(out=gates[:, 0:T], in_=gate[0])
+        nc.sync.dma_start(
             out=gates[:, T:].rearrange("p (r t) -> p r t", r=2), in_=gate[1:TOP, :, TURNED:T].rearrange("r p t -> p r t")
         )
 
@@ -257,7 +259,7 @@ def tile_moe_tk_lin_silu_kernel(
             for r, u in steps:
                 c = (t0 + u) // P
                 m = BLOCKS * (r - 1) + c
-                gated = held.tile([P, P], F32, name=f"gated{r}_{c}")
+                gated = held.tile([P, P], F32, name=f"gated{r}_{c}", tag=f"gated{r}_{c}")
                 nc.scalar.activation(
                     out=gated[:], in_=turned[:, r - 1, u : u + P], func=COPY, scale=gate_columns[:, m : m + 1]
                 )
@@ -271,30 +273,52 @@ def tile_moe_tk_lin_silu_kernel(
                 )
             return back
 
+        def turn_into_sum(bank, part, first, last):
+            for u in range(0, HALF, P):
+                nc.tensor.matmul(
+                    bank[:, u : u + P],
+                    lhsT=part[:, u : u + P],
+                    rhs=identity[:],
+                    is_transpose=True,
+                    start=(first and u == 0),
+                    stop=(last and u == HALF - P),
+                )
+
         result = held.tile([P, T], F32, name="result")
 
-        def store(queue, t0, t1):
-            queue.dma_start(out=out[:, t0:t1], in_=result[:, t0:t1])
+        def store(t0, t1):
+            nc.sync.dma_start(out=out[:, t0:t1], in_=result[:, t0:t1])
 
         ta, tb, tc_, td = 0, HALF, TURNED, TURNED + HALF
         turned_a = fetch_and_turn(ta)
-        turned_b = fetch_and_turn(tb)
+        third_d = fetch_gated(2, td, T)
         second_d = fetch_gated(1, td, T)
-        third_cd = fetch_gated(2, TURNED, T)
-        first = fetch_gated(0, 0, T)
+        first_d = fetch_gated(0, td, T)
+        third_c = fetch_gated(2, tc_, td)
+        first_c = fetch_gated(0, tc_, td)
+        first_ab = fetch_gated(0, ta, tc_)
+        sum_d = psum.tile([P, HALF], F32, name="bank")
+        turn_into_sum(sum_d, third_d, True, False)
+        turn_into_sum(sum_d, second_d, False, False)
+        turn_into_sum(sum_d, first_d, False, True)
+        turned_b = fetch_and_turn(tb)
         back_a = gate_and_turn_back(ta, turned_a)
         plain_c = fetch_plain(1, tc_, td, tag=f"plain2_{ta}")
+        sum_d_turned = held.tile([P, HALF], F32, name="sum_d_turned")
+        nc.scalar.copy(out=sum_d_turned[:], in_=sum_d[:])
+        back_d = psum.tile([P, HALF], F32, name="bank")
+        turn_into_sum(back_d, sum_d_turned, True, True)
         back_b = gate_and_turn_back(tb, turned_b)
-        two_cd = held.tile([P, T - TURNED], F32, name="two_cd")
-        nc.vector.tensor_add(two_cd[:, HALF:], third_cd[:, HALF:], second_d[:])
-        nc.vector.tensor_add(two_cd[:, 0:HALF], third_cd[:, 0:HALF], first[:, tc_:td])
-        nc.vector.tensor_add(result[:, td:T], two_cd[:, HALF:], first[:, td:T])
-        store(nc.sync, td, T)
-        nc.vector.tensor_add(result[:, ta:tb], back_a[:], first[:, ta:tb])
-        store(nc.sync, ta, tb)
+        nc.scalar.copy(out=result[:, td:T], in_=back_d[:])
+        two_c = held.tile([P, HALF], F32, name="two_c")
+        nc.vector.tensor_add(two_c[:], third_c[:], first_c[:])
         second_c = held.tile([P, HALF], F32, name="second_c")
         nc.vector.tensor_tensor(second_c[:], plain_c[:], gates_of(1, tc_, td), MULT)
-        nc.vector.tensor_add(result[:, tb:tc_], back_b[:], first[:, tb:tc_])
-        store(nc.sync, tb, tc_)
-        nc.vector.tensor_add(result[:, tc_:td], two_cd[:, 0:HALF], second_c[:])
-        store(nc.sync, tc_, td)
+        nc.vector.tensor_add(result[:, ta:tb], back_a[:], first_ab[:, ta:tb])
+        store(ta, tb)
+        store(td, T)
+        nc.vector.tensor_add(result[:, tb:tc_], back_b[:], first_ab[:, tb:tc_])
+        store(tb, tc_)
+        result_c = held.tile([P, HALF], F32, name="result_c", tag=f"gated2_{BLOCKS - 1}")
+        nc.vector.tensor_add(result_c[:], two_c[:], second_c[:])
+        nc.sync.dma_start(out=out[:, tc_:td], in_=result_c[:])

@@ -191,7 +191,7 @@ def tile_moe_tk_lin_silu_kernel(
         gather_words(2, S - 2 * GROUP, S - GROUP)
         gather_words(2, S - GROUP, S)
 
-        y = held.tile([P, S], F32, name="y")
+        y = held.tile([P, S], F32, name="y", tag="y")
         def one_pass(acc, a, s0, width):
             e = s0 // C
             cols = slice(s0, s0 + width)
@@ -245,13 +245,10 @@ def tile_moe_tk_lin_silu_kernel(
             nc.scalar.activation(out=plain[:], in_=results_of(r, t0, t1), func=COPY)
             return plain
 
-        def fetch_and_turn(t0):
-            turned = psum_end.tile([P, 2, HALF], F32, name=f"turned{t0}")
-            for r in (1, 2):
-                plain = fetch_plain(r, t0, t0 + HALF)
-                for u in range(0, HALF, P):
-                    nc.tensor.transpose(turned[:, r - 1, u : u + P], plain[:, u : u + P], identity[:])
-            return turned
+        def fetch_and_turn(turned, r, t0):
+            plain = fetch_plain(r, t0, t0 + HALF)
+            for u in range(0, HALF, P):
+                nc.tensor.transpose(turned[:, r - 1, u : u + P], plain[:, u : u + P], identity[:])
 
         def gate_and_turn_back(t0, turned):
             back = psum_end.tile([P, HALF], F32, name=f"back{t0}", tag=f"back{t0}")
@@ -290,7 +287,8 @@ def tile_moe_tk_lin_silu_kernel(
             nc.sync.dma_start(out=out[:, t0:t1], in_=result[:, t0:t1])
 
         ta, tb, tc_, td = 0, HALF, TURNED, TURNED + HALF
-        turned_a = fetch_and_turn(ta)
+        turned_a = psum_end.tile([P, 2, HALF], F32, name="turned_a")
+        turned_b = psum_end.tile([P, 2, HALF], F32, name="turned_b")
         third_d = fetch_gated(2, td, T)
         second_d = fetch_gated(1, td, T)
         first_d = fetch_gated(0, td, T)
@@ -298,27 +296,31 @@ def tile_moe_tk_lin_silu_kernel(
         first_c = fetch_gated(0, tc_, td)
         first_ab = fetch_gated(0, ta, tc_)
         sum_d = psum.tile([P, HALF], F32, name="bank")
+        fetch_and_turn(turned_a, 1, ta)
         turn_into_sum(sum_d, third_d, True, False)
+        fetch_and_turn(turned_a, 2, ta)
         turn_into_sum(sum_d, second_d, False, False)
         turn_into_sum(sum_d, first_d, False, True)
-        turned_b = fetch_and_turn(tb)
+        fetch_and_turn(turned_b, 1, tb)
+        fetch_and_turn(turned_b, 2, tb)
         back_a = gate_and_turn_back(ta, turned_a)
-        plain_c = fetch_plain(1, tc_, td, tag=f"plain2_{ta}")
         sum_d_turned = held.tile([P, HALF], F32, name="sum_d_turned")
         nc.scalar.copy(out=sum_d_turned[:], in_=sum_d[:])
         back_d = psum.tile([P, HALF], F32, name="bank")
         turn_into_sum(back_d, sum_d_turned, True, True)
         back_b = gate_and_turn_back(tb, turned_b)
-        nc.scalar.copy(out=result[:, td:T], in_=back_d[:])
+        plain_c = fetch_plain(1, tc_, td, tag=f"plain2_{tb}")
+        result_d = held.tile([P, HALF], F32, name="result_d", tag=f"gated2_{BLOCKS - 1}")
+        nc.scalar.copy(out=result_d[:], in_=back_d[:])
         two_c = held.tile([P, HALF], F32, name="two_c")
         nc.vector.tensor_add(two_c[:], third_c[:], first_c[:])
-        second_c = held.tile([P, HALF], F32, name="second_c")
-        nc.vector.tensor_tensor(second_c[:], plain_c[:], gates_of(1, tc_, td), MULT)
         nc.vector.tensor_add(result[:, ta:tb], back_a[:], first_ab[:, ta:tb])
         store(ta, tb)
-        store(td, T)
-        nc.vector.tensor_add(result[:, tb:tc_], back_b[:], first_ab[:, tb:tc_])
-        store(tb, tc_)
-        result_c = held.tile([P, HALF], F32, name="result_c", tag=f"gated2_{BLOCKS - 1}")
-        nc.vector.tensor_add(result_c[:], two_c[:], second_c[:])
-        nc.sync.dma_start(out=out[:, tc_:td], in_=result_c[:])
+        nc.sync.dma_start(out=out[:, td:T], in_=result_d[:])
+        second_c = held.tile([P, HALF], F32, name="second_c")
+        nc.vector.tensor_tensor(second_c[:], plain_c[:], gates_of(1, tc_, td), MULT)
+        result_b = held.tile([P, HALF], F32, name="result_b", tag="y")
+        nc.vector.tensor_add(result_b[:], back_b[:], first_ab[:, tb:tc_])
+        nc.sync.dma_start(out=out[:, tb:tc_], in_=result_b[:])
+        nc.vector.tensor_add(result[:, tc_:td], two_c[:], second_c[:])
+        store(tc_, td)

@@ -38,6 +38,7 @@ QUARTER = S // 4
 TURNED = 512
 BLOCKS = TURNED // P
 HALF = 256
+PLAIN = 192
 
 
 def tile_moe_tk_lin_silu_kernel(
@@ -290,16 +291,17 @@ def tile_moe_tk_lin_silu_kernel(
         turned_a = psum_end.tile([P, 2, HALF], F32, name="turned_a")
         turned_b = psum_end.tile([P, 2, HALF], F32, name="turned_b")
         third_d = fetch_gated(2, td, T)
-        second_d = fetch_gated(1, td, T)
+        second_cd = held.tile([P, T - tc_], F32, name="second_cd")
+        te = tc_ + PLAIN
+        nc.vector.tensor_tensor(second_cd[:, PLAIN:], results_of(1, te, T), gates_of(1, te, T), MULT)
         first_d = fetch_gated(0, td, T)
+        first_abc = fetch_gated(0, ta, td)
         third_c = fetch_gated(2, tc_, td)
-        first_c = fetch_gated(0, tc_, td)
-        first_ab = fetch_gated(0, ta, tc_)
         sum_d = psum.tile([P, HALF], F32, name="bank")
         fetch_and_turn(turned_a, 1, ta)
         turn_into_sum(sum_d, third_d, True, False)
         fetch_and_turn(turned_a, 2, ta)
-        turn_into_sum(sum_d, second_d, False, False)
+        turn_into_sum(sum_d, second_cd[:, HALF:], False, False)
         turn_into_sum(sum_d, first_d, False, True)
         fetch_and_turn(turned_b, 1, tb)
         fetch_and_turn(turned_b, 2, tb)
@@ -309,18 +311,17 @@ def tile_moe_tk_lin_silu_kernel(
         back_d = psum.tile([P, HALF], F32, name="bank")
         turn_into_sum(back_d, sum_d_turned, True, True)
         back_b = gate_and_turn_back(tb, turned_b)
-        plain_c = fetch_plain(1, tc_, td, tag=f"plain2_{tb}")
+        plain_c = fetch_plain(1, tc_, te, tag=f"plain2_{tb}")
         result_d = held.tile([P, HALF], F32, name="result_d", tag=f"gated2_{BLOCKS - 1}")
         nc.scalar.copy(out=result_d[:], in_=back_d[:])
-        two_c = held.tile([P, HALF], F32, name="two_c")
-        nc.vector.tensor_add(two_c[:], third_c[:], first_c[:])
-        nc.vector.tensor_add(result[:, ta:tb], back_a[:], first_ab[:, ta:tb])
+        nc.vector.tensor_add(result[:, ta:tb], back_a[:], first_abc[:, ta:tb])
         store(ta, tb)
+        two_c = held.tile([P, HALF], F32, name="two_c", tag=f"gated2_{BLOCKS // 2 - 1}")
+        nc.vector.tensor_add(two_c[:], third_c[:], first_abc[:, tc_:td])
         nc.sync.dma_start(out=out[:, td:T], in_=result_d[:])
-        second_c = held.tile([P, HALF], F32, name="second_c")
-        nc.vector.tensor_tensor(second_c[:], plain_c[:], gates_of(1, tc_, td), MULT)
+        nc.vector.tensor_tensor(second_cd[:, 0:PLAIN], plain_c[:], gates_of(1, tc_, te), MULT)
         result_b = held.tile([P, HALF], F32, name="result_b", tag="y")
-        nc.vector.tensor_add(result_b[:], back_b[:], first_ab[:, tb:tc_])
+        nc.vector.tensor_add(result_b[:], back_b[:], first_abc[:, tb:tc_])
         nc.sync.dma_start(out=out[:, tb:tc_], in_=result_b[:])
-        nc.vector.tensor_add(result[:, tc_:td], two_c[:], second_c[:])
+        nc.vector.tensor_add(result[:, tc_:td], two_c[:], second_cd[:, 0:HALF])
         store(tc_, td)

@@ -312,7 +312,7 @@ def tile_moe_tk_lin_silu_kernel(
         turn_into_sum(back_d, sum_d_turned, True, True)
         back_b = gate_and_turn_back(tb, turned_b)
         plain_c = fetch_plain(1, tc_, te, tag=f"plain2_{tb}")
-        result_d = held.tile([P, HALF], F32, name="result_d", tag=f"gated2_{BLOCKS - 1}")
+        result_d = held.tile([P, HALF], F32, name="result_d", tag=f"gated1_{BLOCKS - 2}")
         nc.scalar.copy(out=result_d[:], in_=back_d[:])
         nc.vector.tensor_add(result[:, ta:tb], back_a[:], first_abc[:, ta:tb])
         store(ta, tb)

from contextlib import ExitStack

import concourse.mybir as mybir
from concourse.masks import make_identity

K, T, E, C, N = 1536, 1024, 12, 256, 128
TOP = 3
S = E * C
PASSES = 3
P = 128
FLOPS = 2 * S * K * N

F32 = mybir.dt.float32
BF16 = mybir.dt.bfloat16
I32 = mybir.dt.int32
U32 = mybir.dt.uint32
U16 = mybir.dt.uint16
U8 = mybir.dt.uint8
FP8X4 = mybir.dt.float8_e4m3fn_x4
FP4X4 = mybir.dt.float4_e2m1fn_x4
COPY = mybir.ActivationFunctionType.Copy
SILU = mybir.ActivationFunctionType.Silu
MULT = mybir.AluOpType.mult

FIRST_ROW = (4, 0, 8)

PIECES = (
    ((512, 256), (256, 128), (128, 128), (128, 0)),
    ((512, 512), (256, 256), (256, 256)),
    ((512, 512), (512, 512)),
)
QUANTISE_WIDTHS = (512, 256, 128)

GROUP = 128
SPACER = 256
EARLY = (S - SPACER, 2048, S)
QUARTER = S // 4
TURNED = 512
BLOCKS = TURNED // P
HALF = 256
PLAIN = 192


def tile_moe_tk_lin_silu_kernel(
    tc, xT, w8_words, w8_scales, w4_words, w4_scales, b, gate, offs, pos1, pos2, pos3, out
):
    nc = tc.nc
    with ExitStack() as ctx:
        held = ctx.enter_context(tc.tile_pool(name="held", bufs=1))
        psum = ctx.enter_context(tc.psum_pool(name="psum", bufs=4))
        psum_end = ctx.enter_context(tc.psum_pool(name="psum_end", bufs=1))

        offs_t = held.tile([P, S // 16], U16, name="offs_t")
        pos_t = [held.tile([P, T // 16], U16, name=f"pos_t{r}") for r in range(TOP)]

        planes = held.tile([P, 4 * T], U8, name="planes", align_bytes=64)
        codes = [held.tile([P, (2 * T, 4 * T, 2 * T)[a]], U32, name=f"codes{a}", align_bytes=64) for a in range(PASSES)]
        moved_plane = held.tile([P, S], U8, name="moved_plane", align_bytes=64)
        w8_plane = held.tile([P, E, N], U8, name="w8_plane", align_bytes=64)
        w4_plane = held.tile([P, 2 * E, N], U8, name="w4_plane", align_bytes=64)
        warm_in = held.tile([P, 1], F32, name="warm_in")
        nc.vector.memset(warm_in[:], 0.0)
        nc.vector.memset(planes[:, 0:T].bitcast(I32), 0)
        for e in range(E):
            nc.vector.memset(w8_plane[:, e, :].bitcast(I32), 0)
        for e in range(0, E, 4):
            nc.vector.memset(w4_plane[:, 2 * e : 2 * e + 8, :].rearrange("p e n -> p (e n)").bitcast(I32), 0)
        nc.vector.memset(moved_plane[:].bitcast(I32), 0)

        warm_out = held.tile([P, 1], F32, name="warm_out")
        nc.scalar.activation(out=warm_out[:], in_=warm_in[:], func=SILU)

        identity = held.tile([P, P], F32, name="identity")
        make_identity(nc, identity[:])
        gate_rows = held.tile([P, P], F32, name="gate_rows")
        nc.gpsimd.memset(gate_rows[:], 0.0)

        raw = {}
        for a in range(PASSES):
            t0 = 0
            for n, on_scalar in PIECES[a]:
                piece = held.tile([P, 4, n], F32, name=f"raw{a}_{t0}", tag=f"raw{a}_{t0}", align_bytes=64)
                nc.sync.dma_start(
                    out=piece[:], in_=xT[512 * a : 512 * a + 512, t0 : t0 + n].rearrange("(p j) t -> p j t", j=4)
                )
                raw[a, t0] = (piece, n, on_scalar)
                t0 = t0 + n
            if a == 0:
                nc.sync.dma_start(offs_t[:], offs)
        for r in (1, 2):
            nc.sync.dma_start(
                out=gate_rows[BLOCKS * (r - 1) : BLOCKS * r, :], in_=gate[r, 0, 0:TURNED].rearrange("(c p) -> c p", p=P)
            )
        gates_turned = psum_end.tile([P, P], F32, name="gates_turned", tag="back0")
        nc.tensor.transpose(gates_turned[:], gate_rows[:], identity[:])
        gate_columns = held.tile([P, 2 * BLOCKS], F32, name="gate_columns")
        nc.scalar.copy(out=gate_columns[:], in_=gates_turned[:, 0 : 2 * BLOCKS])
        for q in range(4):
            nc.sync.dma_start(
                out=w8_plane[32 * q : 32 * q + 4, :, :].bitcast(I32),
                in_=w8_scales[:, 0, 4 * q : 4 * q + 4, :].rearrange("e q n -> q e n").bitcast(I32),
            )
            nc.sync.dma_start(
                out=w4_plane[32 * q : 32 * q + 4, :, :].bitcast(I32),
                in_=w4_scales[:, :, 4 * q : 4 * q + 4, :].rearrange("e a q n -> q (e a) n").bitcast(I32),
            )
        w8 = held.tile([P, E, 4 * N], U8, name="w8", align_bytes=64)
        w4 = held.tile([P, 2 * E, 2 * N], U8, name="w4", align_bytes=64)
        nc.sync.dma_start(
            out=w8[:].bitcast(I32), in_=w8_words.rearrange("e a p n r -> p (e a) (n r)").bitcast(I32)
        )
        nc.sync.dma_start(out=w4[:].bitcast(I32), in_=w4_words.rearrange("e a p m -> p (e a) m").bitcast(I32))
        bias = held.tile([P, E], F32, name="bias")
        nc.sync.dma_start(out=bias[:], in_=b)
        for r, pos in enumerate((pos1, pos2, pos3)):
            nc.sync.dma_start(pos_t[r][:], pos)

        slot_codes = [held.tile([P, EARLY[a]], U32, name=f"slot_codes{a}", align_bytes=64) for a in range(PASSES)]
        slot_planes = held.tile([P, S], U8, name="slot_planes", align_bytes=64)
        held_back = {}

        def round_and_quantise(a):
            for t0 in sorted(t for pass_, t in raw if pass_ == a):
                piece, n, on_scalar = raw[a, t0]
                rounded = held.tile([P, n, 4], BF16, name=f"rounded{a}_{t0}", tag=f"rounded{a}_{t0}", align_bytes=64)
                on_vector = n - on_scalar
                if on_scalar:
                    nc.scalar.activation(
                        out=rounded[:, on_vector:n, :].rearrange("p (c i) j -> p c j i", i=4),
                        in_=piece[:, :, on_vector:n].rearrange("p j (c i) -> p c j i", i=4),
                        func=COPY,
                    )
                if on_vector:
                    nc.vector.tensor_copy(
                        out=rounded[:, 0:on_vector, :].rearrange("p (c i) j -> p c j i", i=4),
                        in_=piece[:, :, 0:on_vector].rearrange("p j (c i) -> p c j i", i=4),
                    )
                u0 = 0
                for share_end in (on_vector, n):
                    for width in QUANTISE_WIDTHS:
                        if u0 + width <= share_end:
                            nc.vector.quantize_mx(
                                out=codes[a][:, t0 + u0 : t0 + u0 + width].bitcast(FP8X4),
                                scales=planes[FIRST_ROW[a] : P, t0 + u0 : t0 + u0 + width],
                                in_=rounded[:, u0 : u0 + width, :].rearrange("p t j -> p (t j)"),
                            )
                            u0 = u0 + width

        def words_of(a, s0, s1):
            width = min(w for w in (T, 2 * T, 4 * T) if 4 * (s1 - s0) <= 3 * w)
            return codes[a][:, 0:width].indirect(offs_t[:, s0 // 16 : s1 // 16])

        def gather_words(a, s0, s1):
            nc.vector.tensor_copy(out=slot_codes[a][:, s0:s1], in_=words_of(a, s0, s1))

        def gather_held_back_words(a, s0, s1, tag, room=None):
            late = held.tile([P, room or s1 - s0], U32, name=f"held_back{a}_{s0}", tag=tag, align_bytes=64)
            nc.vector.tensor_copy(out=late[:, 0 : s1 - s0], in_=words_of(a, s0, s1))
            for s in range(s0, s0 + (room or s1 - s0), GROUP):
                held_back[a, s] = (late, s - s0)

        def gather_scale_bytes(s0, s1):
            nc.vector.tensor_copy(out=slot_planes[:, s0:s1], in_=planes[:].indirect(offs_t[:, s0 // 16 : s1 // 16]))
            for q in range(4):
                row = 32 * q + FIRST_ROW[2]
                nc.sync.dma_start(
                    out=moved_plane[32 * q : 32 * q + 4, s0:s1].bitcast(I32),
                    in_=slot_planes[row : row + 4, s0:s1].bitcast(I32),
                )

        round_and_quantise(0)
        gather_words(0, 0, S // 2)
        gather_words(0, S // 2, EARLY[0])
        round_and_quantise(1)
        gather_held_back_words(0, EARLY[0], S, "raw1_768")
        gather_words(1, 0, EARLY[1])
        round_and_quantise(2)
        gather_held_back_words(1, EARLY[1], S - C, "raw2_512")

        gates = held.tile([P, T + 2 * (T - TURNED)], F32, name="gates", tag="rounded2_0", align_bytes=64)
        nc.sync.dma_start(out=gates[:, 0:T], in_=gate[0])
        nc.sync.dma_start(
            out=gates[:, T:].rearrange("p (r t) -> p r t", r=2), in_=gate[1:TOP, :, TURNED:T].rearrange("r p t -> p r t")
        )

        gather_scale_bytes(0, EARLY[1])
        gather_words(2, 0, S // 2)
        gather_scale_bytes(EARLY[1], S)
        gather_words(2, 2 * QUARTER, 3 * QUARTER)
        gather_words(2, 3 * QUARTER, S - C)
        gather_held_back_words(1, S - C, S, "rounded2_512")
        gather_words(2, S - 2 * GROUP, S - GROUP)
        gather_words(2, S - GROUP, S)

        y = held.tile([P, S], F32, name="y", tag="y")
        def one_pass(acc, a, s0, width):
            e = s0 // C
            cols = slice(s0, s0 + width)
            if a == 0:
                weights, weight_plane = w8[:, e, :].bitcast(FP8X4), w8_plane[:, e, :]
            else:
                m = 2 * e + a - 1
                weights, weight_plane = w4[:, m, :].bitcast(FP4X4), w4_plane[:, m, :]
            if s0 < EARLY[a]:
                words = slot_codes[a][:, cols]
            else:
                late, u = held_back[a, s0]
                words = late[:, u : u + width]
            nc.tensor.matmul_mx(
                out=acc[:],
                lhsT=weights,
                lhsT_scale=weight_plane,
                rhs=words.bitcast(FP8X4),
                rhs_scale=moved_plane[:, cols] if a == 2 else slot_planes[FIRST_ROW[a] : P, cols],
                start=(a == 0),
                stop=(a == PASSES - 1),
            )

        groups = [(s, C) for s in range(0, S - C, C)] + [(s, GROUP) for s in range(S - C, S, GROUP)]
        for q0, q1 in ((0, QUARTER), (QUARTER, 2 * QUARTER), (2 * QUARTER, 3 * QUARTER), (3 * QUARTER, S - C), (S - C, S)):
            mine = [(s0, width) for s0, width in groups if q0 <= s0 < q1]
            acc = {s0: psum.tile([P, width], F32, name="bank") for s0, width in mine}
            for a in range(PASSES - 1):
                for s0, width in mine:
                    one_pass(acc[s0], a, s0, width)
            for s0, width in mine:
                one_pass(acc[s0], PASSES - 1, s0, width)
                nc.scalar.activation(
                    out=y[:, s0 : s0 + width], in_=acc[s0][:], func=SILU, bias=bias[:, s0 // C : s0 // C + 1]
                )

        def results_of(r, t0, t1):
            return y[:].indirect(pos_t[r][:, t0 // 16 : t1 // 16])

        def gates_of(r, t0, t1):
            first = T + (r - 1) * (T - TURNED) - TURNED if r else 0
            return gates[:, first + t0 : first + t1]

        def fetch_gated(r, t0, t1):
            part = held.tile([P, t1 - t0], F32, name=f"part{r}_{t0}")
            nc.vector.tensor_tensor(part[:], results_of(r, t0, t1), gates_of(r, t0, t1), MULT)
            return part

        def fetch_plain(r, t0, t1, tag=None):
            plain = held.tile([P, t1 - t0], F32, name=f"plain{r}_{t0}", tag=tag or f"plain{r}_{t0}")
            nc.scalar.activation(out=plain[:], in_=results_of(r, t0, t1), func=COPY)
            return plain

        def fetch_and_turn(turned, r, t0):
            plain = fetch_plain(r, t0, t0 + HALF)
            for u in range(0, HALF, P):
                nc.tensor.transpose(turned[:, r - 1, u : u + P], plain[:, u : u + P], identity[:])

        def gate_and_turn_back(t0, turned):
            back = psum_end.tile([P, HALF], F32, name=f"back{t0}", tag=f"back{t0}")
            steps = [(r, u) for r in (1, 2) for u in range(0, HALF, P)]
            for r, u in steps:
                c = (t0 + u) // P
                m = BLOCKS * (r - 1) + c
                gated = held.tile([P, P], F32, name=f"gated{r}_{c}", tag=f"gated{r}_{c}")
                nc.scalar.activation(
                    out=gated[:], in_=turned[:, r - 1, u : u + P], func=COPY, scale=gate_columns[:, m : m + 1]
                )
                nc.tensor.matmul(
                    back[:, u : u + P],
                    lhsT=gated[:],
                    rhs=identity[:],
                    is_transpose=True,
                    start=((r, u) == steps[0]),
                    stop=((r, u) == steps[-1]),
                )
            return back

        def turn_into_sum(bank, part, first, last):
            for u in range(0, HALF, P):
                nc.tensor.matmul(
                    bank[:, u : u + P],
                    lhsT=part[:, u : u + P],
                    rhs=identity[:],
                    is_transpose=True,
                    start=(first and u == 0),
                    stop=(last and u == HALF - P),
                )

        result = held.tile([P, T], F32, name="result")

        def store(t0, t1):
            nc.sync.dma_start(out=out[:, t0:t1], in_=result[:, t0:t1])

        ta, tb, tc_, td = 0, HALF, TURNED, TURNED + HALF
        turned_a = psum_end.tile([P, 2, HALF], F32, name="turned_a")
        turned_b = psum_end.tile([P, 2, HALF], F32, name="turned_b")
        third_d = fetch_gated(2, td, T)
        second_cd = held.tile([P, T - tc_], F32, name="second_cd")
        te = tc_ + PLAIN
        nc.vector.tensor_tensor(second_cd[:, PLAIN:], results_of(1, te, T), gates_of(1, te, T), MULT)
        first_d = fetch_gated(0, td, T)
        first_abc = fetch_gated(0, ta, td)
        third_c = fetch_gated(2, tc_, td)
        sum_d = psum.tile([P, HALF], F32, name="bank")
        fetch_and_turn(turned_a, 1, ta)
        turn_into_sum(sum_d, third_d, True, False)
        fetch_and_turn(turned_a, 2, ta)
        turn_into_sum(sum_d, second_cd[:, HALF:], False, False)
        turn_into_sum(sum_d, first_d, False, True)
        fetch_and_turn(turned_b, 1, tb)
        fetch_and_turn(turned_b, 2, tb)
        back_a = gate_and_turn_back(ta, turned_a)
        sum_d_turned = held.tile([P, HALF], F32, name="sum_d_turned")
        nc.scalar.copy(out=sum_d_turned[:], in_=sum_d[:])
        back_d = psum.tile([P, HALF], F32, name="bank")
        turn_into_sum(back_d, sum_d_turned, True, True)
        back_b = gate_and_turn_back(tb, turned_b)
        plain_c = fetch_plain(1, tc_, te, tag=f"plain2_{tb}")
        result_d = held.tile([P, HALF], F32, name="result_d", tag=f"gated1_{BLOCKS - 2}")
        nc.scalar.copy(out=result_d[:], in_=back_d[:])
        nc.vector.tensor_add(result[:, ta:tb], back_a[:], first_abc[:, ta:tb])
        store(ta, tb)
        two_c = held.tile([P, HALF], F32, name="two_c", tag=f"gated2_{BLOCKS // 2 - 1}")
        nc.vector.tensor_add(two_c[:], third_c[:], first_abc[:, tc_:td])
        nc.sync.dma_start(out=out[:, td:T], in_=result_d[:])
        nc.vector.tensor_tensor(second_cd[:, 0:PLAIN], plain_c[:], gates_of(1, tc_, te), MULT)
        result_b = held.tile([P, HALF], F32, name="result_b", tag="y")
        nc.vector.tensor_add(result_b[:], back_b[:], first_abc[:, tb:tc_])
        nc.sync.dma_start(out=out[:, tb:tc_], in_=result_b[:])
        nc.vector.tensor_add(result[:, tc_:td], two_c[:], second_cd[:, 0:HALF])
        store(tc_, td)
